import numpy as np, ml_dtypes
CORES = [48,51,52,55]
N = 4
BF = ml_dtypes.bfloat16
W, C, RO, SH = 4096, 256, 6, 4
def parts(rng):
    cov = np.where(rng.random((N, 8, 1, W)) < 0.15, 0, rng.integers(0, 256, (N, 8, 16, W)))
    share = rng.choice(np.array([0.0, 0.1, 0.2, 0.3, 0.5, 0.8]), (N, 8, 1, C))
    tst = np.where(rng.random((N, 8, 16, C)) < share, 256, rng.integers(0, 256, (N, 8, 16, C)))
    return cov, tst, rng.integers(0, 160, (N, 8, 16, C)), rng.integers(200, 2000, (N, 8))
def pack(cov, tst, pr, th):
    return {"cov": np.ascontiguousarray(cov.reshape(N, 128, W)).astype(np.float32).astype(BF), "tst": np.ascontiguousarray(tst.reshape(N, 128, C)).astype(np.int32),
            "pr": np.ascontiguousarray(pr.reshape(N, 128, C)).astype(np.float32).astype(BF), "th": np.ascontiguousarray(th.reshape(N, 8, 1)).astype(np.int32)}
def setup_inputs(rng):
    return pack(*parts(rng))
def setup_inputs_corners(rng):
    cov, tst, pr, th = parts(rng)
    c = np.arange(C); lane = np.arange(16)[:, None]; full = rng.integers(0, 256, (N, 8, 16, C))
    th = rng.choice(np.array([0, 1, 500, 4080]), (N, 8))
    for r in range(N):
        for g in range(8):
            k = (g + r) % 8; x = full[r, g]
            if k == 1: x = np.full((16, C), 256)
            elif k == 2: x = np.where(lane == c % 16, 256, x)
            elif k == 3: x = np.where((lane + c) % 2 == 1, 256, x)
            elif k == 4:
                x = np.repeat(x[:, :1], C, axis=1); pr[r, g] = np.repeat(pr[r, g][:, :1], C, axis=1); th[r, g] = 0
            elif k == 5: x = np.where((lane == c % 16) | (lane == (c + 1) % 16), x, 256)
            elif k == 6:
                cov[r, g][:, rng.random(W) < 0.7] = 0; th[r, g] = 0
            elif k == 7: pr[r, g] = 255 * rng.integers(0, 2, (1, C))
            tst[r, g] = x
    q = rng.permutation(N); th[q[0]] = 0; th[q[1]] = 4080
    r = int(q[0]); g = (8 - r) % 8
    cov[r, g, 0] = 0; cov[r, g, 1:] = rng.integers(1, 256, (15, W))
    pr[r, g, :, 0::2] = 255; pr[r, g, :, 1::2] = 0
    k = np.arange(C // 2); p = 1 + k % 14; v = rng.integers(0, 256, (2, C // 2)); x = np.full((16, C), 256)
    for odd in range(2):
        x[p, 2 * k + odd] = v[0]; x[p + 1, 2 * k + odd] = v[1]
    tst[r, g] = x
    return pack(cov, tst, pr, th)
def pairs(rng, low):
    x = rng.integers(0, 256, 2 ** 15); y = rng.integers(0, 256, 2 ** 15); i = rng.integers(0, 16, 2 ** 15)
    col, at = np.unique(((((2 * x + 1) * (2 * y + 1)) >> 4) + 613 * i) & (W - 1), return_index=True)
    at = rng.permutation(at[col >= low])
    return x[at], y[at], i[at]
def lone(rng, x, y, i):
    k = len(x); c = np.arange(k); v = np.full((16, k), 256)
    v[i, c] = x; v[(i + 1) & 15, c] = y
    for d in range(3, 15, 2): v[(i + d) & 15, c] = rng.integers(0, 256, k)
    return v
def setup_inputs_crowd(rng):
    cov, tst, pr, th = parts(rng)
    a = int(rng.integers(0, N)); b = (a + 1) % N; d = (a + 2) % N
    v = rng.integers(0, 256, (8, 16, C)); v[:, [1, 5, 7, 9, 11, 13, 15]] = 256
    tst[a] = v; th[a] = rng.integers(511, 1500, 8); th[b] = 0; th[d] = 0
    cov[b] = rng.integers(1, 256, (8, 16, W)); cov[d] = rng.integers(1, 256, (8, 16, W))
    c = np.arange(C); second = ((c % 2 == 0) & (c > 0)) | (c == C - 1)
    for g in range(8):
        p = np.append(rng.permutation(C - 1)[:31], C - 1)
        few = ((((2 * v[g, 2, p] + 1) * (2 * v[g, 3, p] + 1)) >> 4) + 613 * 2) & (W - 1)
        most = ((((2 * v[g, 3, p] + 1) * (2 * v[g, 4, p] + 1)) >> 4) + 613 * 3) & (W - 1)
        cov[a, g][:, few] = 255; cov[a, g][int(rng.integers(0, 16)), few] = 254; cov[a, g][:, most] = 255
        x, y, i = pairs(rng, 0)
        tst[b, g] = lone(rng, x[:C], y[:C], i[:C])
        x, y, i = pairs(rng, W - 254 if g == 7 else 0)
        o = (c + 1) // 2; o[C - 1] = 0; o = np.where(o > 0, 1 + (o - 1) % (len(x) - 1), 0)
        tst[d, g] = lone(rng, x[o], y[o], i[o])
        lev = rng.integers(0, 16, C // 2)[o]; lev = np.where(second, (lev + rng.integers(1, 16, C)) & 15, lev)
        pr[d, g] = np.where(np.arange(16)[:, None] == lev[None, :], 0, 255)
    return pack(cov, tst, pr, th)
def setup_inputs_ties(rng):
    unit = np.where(np.arange(8) % 4 == 1, 1, 85).reshape(1, 8, 1, 1)
    cov = unit * np.where(rng.random((N, 8, 1, W)) < 0.5, rng.integers(0, 4, (N, 8, 1, W)), rng.integers(0, 4, (N, 8, 16, W)))
    pr = unit * np.where(rng.random((N, 8, 1, C)) < 0.5, rng.integers(0, 2, (N, 8, 1, C)), rng.integers(0, 2, (N, 8, 16, C)))
    few = rng.choice(np.array([0, 1, 64, 128, 255, 256]), (N, 8, 16, C)); many = np.where(rng.random((N, 8, 16, C)) < 0.2, 256, rng.integers(0, 256, (N, 8, 16, C)))
    tst = np.where(rng.random((N, 8, 1, C)) < 0.5, few, many)
    return pack(cov, tst, pr, unit[..., 0, 0] * rng.integers(0, 24, (N, 8)))
def setup_inputs_spread(rng):
    cov = np.minimum((np.exp2(8 * rng.random((N, 8, 1, W))) * rng.random((N, 8, 16, W)) * 1.01).astype(np.int64), 255)
    pr = np.minimum((np.exp2(8 * rng.random((N, 8, 16, C))) * rng.random((N, 8, 1, C))).astype(np.int64), 255)
    tst = np.minimum((256 * rng.random((N, 8, 16, C)) ** rng.choice(np.array([0.25, 1.0, 4.0]), (N, 8, 16, 1))).astype(np.int64), 255)
    tst = np.where(rng.random((N, 8, 16, C)) < rng.random((N, 8, 1, C)) * 0.6, 256, tst)
    th = np.minimum(np.exp2(12 * rng.random((N, 8))).astype(np.int64) - 1, 4080)
    return pack(cov, tst, pr, th)
def setup_inputs_ends(rng):
    kind = rng.integers(0, 3, (N, 8, 1, W)); cov = 255 * np.where(kind == 2, rng.integers(0, 2, (N, 8, 16, W)), kind)
    lane = np.arange(16)
    for t in range(RO):
        z = (613 * lane + 77 * t) & (W - 1); f = ((511 * 511 >> 4) + 613 * lane + 77 * t) & (W - 1)
        cov[..., z] = 255; cov[..., f] = 0; cov[..., f[15]] = 255; cov[:, ::2, :, f[6]] = 255
    u = rng.random((N, 8, 16, C))
    tst = np.where(u < 0.5, 0, np.where(u < 0.7, 256, np.where(u < 0.9, 255, rng.integers(0, 256, (N, 8, 16, C)))))
    tst[..., [2, C - 1]] = 0; tst[..., [5, C - 2]] = 255; tst[..., [1, C - 3]] = 256
    pr = 255 * rng.integers(0, 2, (N, 8, 16, C))
    pr[..., [2, 5, C - 2, C - 1]] = 255; pr[:, :, 15, [2, 5, C - 2, C - 1]] = 0; pr[:, 1::2, 4, [2, C - 1]] = 0
    o = np.argsort(rng.random((N, 8)), axis=1); th = 4080 * (o < rng.integers(3, 6, (N, 1))).astype(np.int64)
    th[N - 1, 7] = 4080; th[N - 1, 0] = 0
    return pack(cov, tst, pr, th)
def check_inputs(d):
    bad = []
    for k, lo, hi in (("cov", 0, 255), ("tst", 0, 256), ("pr", 0, 255), ("th", 0, 4080)):
        v = np.asarray(d[k]).astype(np.float64)
        if not (np.min(v) >= lo and np.max(v) <= hi): bad.append("range of " + k)
        elif np.any(v != np.floor(v)): bad.append("whole numbers in " + k)
    return bad
def reference(cov, tst, pr, th):
    U = cov.astype(np.float32).astype(np.int64).reshape(N, 8, 16, W); T = tst.astype(np.int64).reshape(N, 8, 16, C)
    price = pr.astype(np.float32).astype(np.int64).reshape(N, 8, 16, C); lim = th.astype(np.int64).reshape(N, 8, 1)
    lane = np.arange(16).reshape(1, 16, 1); last = np.zeros(N, np.int64)
    for t in range(RO):
        rho = (5 * t) & 15; now = np.zeros(N, np.int64)
        for r in range(N):
            s = (r + t) % N
            x = T[r]; y = np.roll(x, -(1 + t), axis=1)
            live = (x != 256) & (y != 256)
            code = ((((2 * x + 1) * (2 * y + 1)) >> 4) + 613 * lane + 77 * t) & (W - 1)
            got = np.take_along_axis(U[s], code.reshape(8, 1, 16 * C), 2).reshape(8, 16, 16, C)
            gain = np.add.reduce(np.where(live[:, None], np.maximum(got - price[s][:, :, None, :], 0), 0), axis=2)
            lev = np.argmax(gain, axis=1); best = np.max(gain, axis=1)
            useful = best >= lim[s] + (last[s] & 255); now[s] = np.sum(~useful)
            some = np.any(live, axis=1)
            vote = np.argmax(np.where(live, np.add.reduce(got, axis=1), -1), axis=1)
            taken = np.take_along_axis(code, vote[:, None, :], 1)[:, 0] >> SH
            most = np.argmax(np.where(live, np.take_along_axis(got, lev[:, None, None, :], 1)[:, 0], -1), axis=1)
            credit = np.take_along_axis(code, most[:, None, :], 1)[:, 0]
            none = x == 256; first = np.argmax(none, axis=1)
            new = np.array(x)
            g, c = np.nonzero(~useful & some & np.any(none, axis=1))
            new[g, first[g, c], c] = taken[g, c]
            new[:, rho] = np.where(useful, 16 * lev + (best & 15), 256)
            for g in range(8):
                c = np.nonzero(useful[g] & some[g])[0]
                col, at = np.unique(credit[g, c], return_index=True)
                U[s, g, lev[g, c[at]], col] = 0
            T[r] = new
        last = now
    left = np.add.reduce(U.reshape(N, 128, W // 16, 16), axis=3)
    return {"yt": T.reshape(N, 128, C).astype(np.float32), "yc": left.astype(np.float32)}

@@ -1,0 +1,503 @@
+from concourse.mybir import AluOpType as A, AxisListType, ActivationFunctionType as F
+
+N = 4
+RO = 6
+C = 256
+W = 4096
+UW = 4368
+VOID = 4096
+DUMMY = 4112
+FLAG = 2.0 ** 19
+BIG = 2.0 ** 20
+CH = 4
+S_RED = [(a, b) for a in range(4) for b in range(4) if b != 1 and (a, b) not in ((3, 3), (3, 0))]
+RHO = [(5 * t) % 16 for t in range(RO)]
+
+SCRATCH = {}
+for _n, _w, _d in [
+    ("U", UW, "bfloat16"), ("PXP", W, "bfloat16"), ("R", W, "bfloat16"), ("M", W, "bfloat16"), ("PR", W, "bfloat16"),
+    ("P", C, "bfloat16"), ("TI", C, "int32"), ("NF", C, "bfloat16"), ("FN", C, "bfloat16"), ("QF", C, "float32"),
+    ("FI", C, "int32"), ("XI", C, "int32"), ("OFF", C, "uint16"), ("CM", C, "float32"), ("MG", C, "float32"), ("N4", C, "bfloat16"),
+    ("KT", C, "float32"), ("S1", C, "float32"), ("VT", C, "float32"), ("S2", C, "float32"), ("XT", C, "float32"), ("S3", C, "float32"),
+    ("WT", C, "float32"), ("W1", C, "bfloat16"), ("EA", C, "bfloat16"), ("EN", C, "bfloat16"), ("EB", C, "bfloat16"), ("VN", C, "bfloat16"),
+    ("VM", 2 * C, "bfloat16"), ("RV", C, "bfloat16"), ("JK", C, "bfloat16"), ("DL", C, "bfloat16"), ("NV", C, "bfloat16"),
+    ("TAU", 16, "int32"), ("LB", 16, "float32"), ("KV", 16, "int32"), ("NB", 16, "int32"), ("TK", 16, "float32"), ("ZV", 16, "float32"),
+    ("X1", 16, "int32"), ("X2", 16, "int32"), ("KI", 16, "int32"), ("D0", 16, "int32"), ("D1", 16, "int32"), ("D2", 16, "int32"),
+    ("ZK", 16, "float32"), ("ZZ", 16, "float32"), ("XC", 16, "int32"), ("XF", 16, "float32"), ("XL", 16, "float32"), ("YL", 16, "float32"), ("YM", 16, "float32"),
+    ("OL", 16, "uint16"), ("FL", 16, "float32"), ("FB", 64, "bfloat16"), ("LIM", 16, "float32"), ("TH16", 16, "float32"), ("THI", 1, "int32"),
+    ("THF", 1, "float32"), ("TH8", 16, "float32"), ("MC", 1, "float32"), ("MA", 1, "float32"), ("MQ", 1, "float32"), ("MR", 1, "float32"), ("MF", 1, "float32"), ("MJK", 16, "float32"), ("UG", C, "bfloat16"),
+    ("OUTT", C, "float32"), ("OUTC", C, "float32"),
+    ("cM", 128, "int32"), ("cD", 128, "int32"), ("cJ", 128, "int32"), ("cT", 128, "int32"), ("cG", 16, "int32"), ("cH", 16, "int32"),
+    ("cP", 1, "int32"), ("cI", 8, "int32"), ("cF", 64, "float32"), ("cBM", 128, "bfloat16"), ("cMI", 128, "bfloat16"), ("cDD", 128, "bfloat16"), ("cDM", 128, "bfloat16"),
+    ("cA", 128, "bfloat16"), ("cB", 128, "bfloat16"), ("mI", 128, "bfloat16"), ("mI16", 128, "bfloat16"), ("mP256", 128, "bfloat16"), ("mIF", 128, "float32"),
+    ("mPT", 128 * RO, "bfloat16"), ("mQT", 128 * RO, "bfloat16"), ("mKC", 128 * RO, "bfloat16"), ("iKC", 128 * RO, "int32"), ("jKC", 128 * RO, "int32"),
+    ("mE", 2048, "bfloat16"), ("mEX", 2048, "bfloat16"), ("mCH", 128, "bfloat16"), ("mCV", 128, "bfloat16"), ("mCX", 128, "bfloat16"),
+    ("mFN", 128, "bfloat16"), ("mBR", 128 * RO, "bfloat16"), ("mNR", 128 * RO, "bfloat16"), ("mB0", 128, "bfloat16"), ("mON", C, "bfloat16"),
+    ("mXX", 128, "bfloat16"), ("mLM", 512, "bfloat16"), ("mLX", 512, "float32"), ("mTH", 128, "float32"),
+    ("cMASK", C, "float32"), ("cNEG", C, "float32"), ("cBL", 16, "uint16"), ("cDUM", 16, "float32"), ("TS", C * RO, "bfloat16"),
+]:
+    SCRATCH[_n] = ("sbuf", [128, _w], _d)
+for _t in range(RO + 1):
+    SCRATCH["TB%d" % _t] = ("sbuf", [128, C], "bfloat16")
+for _b in range(8):
+    SCRATCH["bk%d" % _b] = ("psum", [128, 512], "float32")
+SEMAPHORES = ["v", "s", "p", "g", "snd"] + ["arr%d" % t for t in range(1, RO + 1)] + ["dma%d" % k for k in range(8)]
+
+
+def rank_program(g, core, T, topo):
+    rank = T.rank_of(core)
+    if rank is None:
+        return
+    queue = {"v": g.vector, "s": g.scalar, "p": g.tensor, "g": g, "y": g.sync}
+    count = {}
+    known = {q: {} for q in queue}
+    done = {}
+    last = {}
+
+    def need(q, sem, val):
+        if known[q].get(sem, 0) >= val:
+            return
+        queue[q].wait_ge(T.sem[sem], val)
+        known[q][sem] = val
+        for k, x in done.get((sem, val), {}).items():
+            if known[q].get(k, 0) < x:
+                known[q][k] = x
+
+    def spans(views):
+        out = []
+        for x in views:
+            if isinstance(x, str):
+                x = (x, 0, 1 << 20)
+            out.append(x)
+        return out
+
+    def order(q, reads, writes, sem, val):
+        todo = {}
+        reads, writes = spans(reads), spans(writes)
+        for views, wr in ((reads, False), (writes, True)):
+            for b, lo, hi in views:
+                bank = b.startswith("bk")
+                for l2, h2, w2, q2, s2, v2 in last.get(b, []):
+                    if bank:
+                        hit = q2 != q or (w2 and q != "p")
+                    else:
+                        hit = (wr or w2) and l2 < hi and lo < h2
+                    if hit and todo.get(s2, 0) < v2:
+                        todo[s2] = v2
+        for s2, v2 in sorted(todo.items(), key=lambda kv: -sum(done.get(kv, {}).values())):
+            need(q, s2, v2)
+        return reads, writes
+
+    def note(q, reads, writes, sem, val):
+        for views, wr in ((reads, False), (writes, True)):
+            for b, lo, hi in views:
+                bank = b.startswith("bk")
+                keep = []
+                for e in last.get(b, []):
+                    if bank:
+                        if e[3] == q and (wr or not e[2]):
+                            continue
+                        if e[3] != q:
+                            continue
+                    elif wr and lo <= e[0] and e[1] <= hi:
+                        continue
+                    elif not wr and not e[2] and e[3] == q and lo <= e[0] and e[1] <= hi:
+                        continue
+                    keep.append(e)
+                keep.append((lo, hi, wr, q, sem, val))
+                last[b] = keep
+        know = dict(known[q])
+        know[sem] = val
+        done[(sem, val)] = know
+
+    def run(q, call, reads, writes):
+        val = count.get(q, 0) + 1
+        reads, writes = order(q, reads, writes, q, val)
+        call(queue[q]).then_inc(T.sem[q], 1)
+        count[q] = val
+        note(q, reads, writes, q, val)
+
+    def dma(q, k, out, in_, reads, writes):
+        sem = "dma%d" % k
+        reads, writes = order(q, reads, writes, sem, 16)
+        queue[q].dma_start(out, in_).then_inc(T.sem[sem], 16)
+        note(q, reads, writes, sem, 16)
+
+    def arrive(buf, sem, val):
+        last[buf] = [(0, 1 << 20, True, "r", sem, val)]
+
+    def V(name, out, wr, rd, *a, **k):
+        run("v", lambda e: {"tt": e.tensor_tensor, "ts": e.tensor_scalar, "cp": e.tensor_copy, "tr": e.transpose, "sc": e.tensor_tensor_scan,
+                            "rd": e.tensor_reduce, "ms": e.memset}[name](out, *a, **k), rd, wr)
+
+    def S(out, in_, wr, rd, func=F.Identity, **k):
+        run("s", lambda e: e.activation(out, in_, func, **k), rd, wr)
+
+    def MM(out, lhsT, rhs, start, stop, bank, rd):
+        run("p", lambda e: e.matmul(out, lhsT, rhs, start, stop), rd, [bank])
+
+    def col(k):
+        return T.cF[:, k:k + 1]
+
+    def ts(out, wr, in0, rd, s1, s2, op0, op1=None):
+        if op1 is None:
+            V("ts", out, wr, rd, in0, s1, None, op0)
+        else:
+            V("ts", out, wr, rd, in0, s1, s2, op0, op1)
+
+    def tt(out, wr, a, b, rd, op):
+        V("tt", out, wr, rd, a, b, op)
+
+    EAS = ["EA%d" % r for r in range(5)]
+    E16 = lambda r: slice(r, C, 16)
+
+    dma("y", 0, T.TI[:], T.tst[:], [], ["TI"])
+    dma("s", 1, T.P[:], T.pr[:], [], ["P"])
+    dma("s", 2, T.THI[0:8, :], T.th[:], [], ["THI"])
+    dma("y", 3, T.U[:, 0:W], T.cov[:], [], [("U", 0, W)])
+
+    def iota(name, pattern, base, cm):
+        run("g", lambda e: e.iota(T[name][:], pattern, base, cm), [], [name])
+    iota("cD", [[1, 128]], 256, -1)
+    iota("cM", [[1, 128]], 0, 0)
+    iota("cP", [[0, 1]], 0, 1)
+    iota("iKC", [[77, RO], [0, 8], [613, 16]], 0, 0)
+    iota("cG", [[1, 16]], 0, 0)
+
+    V("ms", T.U[:, W:UW], [("U", W, UW)], [], -1.0)
+    V("ms", T.mON[:], ["mON"], [], 1.0)
+    for k, x in ((60, -511.0 * FLAG), (61, 1.5 * 2.0 ** 23), (62, -1.5 * 2.0 ** 23), (63, -127.5)):
+        V("ms", T.cF[:, k:k + 1], [("cF", k, k + 1)], [], x)
+    def sh(name, src, ops, lo=0, hi=128):
+        if len(ops) == 1:
+            ts(name[0][:], [name[1]], src[0][:], [src[1]], ops[0][1], None, ops[0][0])
+        else:
+            ts(name[0][:], [name[1]], src[0][:], [src[1]], ops[0][1], ops[1][1], ops[0][0], ops[1][0])
+    AND, SHR = A.bitwise_and, A.arith_shift_right
+    def icol(k, ops, op2=None):
+        if len(ops) == 1:
+            ts(T.cI[:, k:k + 1], [("cI", k, k + 1)], T.cP[:], ["cP"], ops[0][1], None, ops[0][0])
+        else:
+            ts(T.cI[:, k:k + 1], [("cI", k, k + 1)], T.cP[:], ["cP"], ops[0][1], ops[1][1], ops[0][0], ops[1][0])
+    icol(0, [(SHR, 4)])
+    icol(1, [(AND, 15)])
+    icol(2, [(SHR, 4), (AND, 1)])
+    icol(3, [(AND, 1)])
+    icol(4, [(AND, 31), (SHR, 1)])
+    icol(5, [(SHR, 1)])
+    icol(6, [(SHR, 5)])
+    V("cp", T.cF[:, 0:7], [("cF", 0, 7)], ["cI"], T.cI[:, 0:7])
+
+    def fcol(k, src, s1, s2, op0, op1=None):
+        ts(col(k), [("cF", k, k + 1)], col(src), [("cF", src, src + 1)], s1, s2, op0, op1)
+
+    ts(T.cJ[:], ["cJ"], T.cM[:], ["cM"], 4, None, SHR)
+    ts(T.cBM[:], ["cBM"], T.cJ[:], ["cJ", ("cF", 0, 1)], col(0), None, A.is_equal)
+    ts(T.cA[:], ["cA"], T.cBM[:], ["cBM"], -100.0, 100.0, A.mult, A.add)
+    ts(T.cT[:], ["cT"], T.cD[:], ["cD"], 15, None, AND)
+    ts(T.cB[:], ["cB"], T.cT[:], ["cT"], 1.0, None, A.mult)
+    tt(T.cDD[:], ["cDD"], T.cB[:], T.cA[:], ["cA", "cB"], A.add)
+    def eqm(name, c0, val, scale):
+        ts(T[name][:, c0:c0 + 128], [(name, c0, c0 + 128)], T.cDD[:], ["cDD"], float(val), float(scale), A.is_equal, A.mult)
+    eqm("mI", 0, 0, 1)
+
+    def const_t(t):
+        eqm("mPT", 128 * t, (-(1 + t)) % 16, 1)
+        tt(T.mQT[:, 128 * t:128 * t + 128], [("mQT", 128 * t, 128 * t + 128)], T.mPT[:, 128 * t:128 * t + 128], T.mI[:], [("mPT", 128 * t, 128 * t + 128), "mI"], A.add)
+        x = slice(128 * t, 128 * t + 128)
+        for p0, nm, bits, add in ((0, "KCa%d" % t, 4080, 0.0), (64, "KCb%d" % t, 15, 1.0 / 64)):
+            ts(T.jKC[p0:p0 + 64, x], ["j" + nm], T.iKC[p0:p0 + 64, x], ["iKC"], bits, None, AND)
+            ts(T.mKC[p0:p0 + 64, x], [nm], T.jKC[p0:p0 + 64, x], ["j" + nm], 0.25, add, A.mult, A.add)
+
+    def const_r(t):
+        rho = RHO[t]
+        if t:
+            fcol(10 + t, 1, float(rho), 1.0 / FLAG, A.not_equal, A.mult)
+        ts(T.mBR[:, 128 * t:128 * t + 128], [("mBR", 128 * t, 128 * t + 128)], T.mE[:, 128 * rho:128 * rho + 128], [("mE", 128 * rho, 128 * rho + 128), ("cF", 20, 21)], col(20), None, A.mult)
+        ts(T.mNR[:, 128 * t:128 * t + 128], [("mNR", 128 * t, 128 * t + 128)], T.mI[:], ["mI", ("cF", 10 + t, 11 + t)], col(10 + t), FLAG, A.mult, A.mult)
+    const_t(0)
+    ts(T.TB0[:], ["TB0"], T.TI[:], ["TI"], 2.0, None, A.mult)
+
+    def codes(t):
+        TB = "TB%d" % t
+        tb = T[TB]
+        S(T.NF[:], tb[:], ["NF"], [TB, ("cF", 60, 63)], F.Relu, scale=FLAG, bias=col(60))
+        MM(T.bk0[:, 0:C], T.mPT[:, 128 * t:128 * t + 128], tb[:], True, True, "bk0", [("mPT", 128 * t, 128 * t + 128), TB])
+        q = T.mQT[:, 128 * t:128 * t + 128]
+        MM(T.bk1[:, 0:C], T.mKC[:, 128 * t:128 * t + 128], T.mON[:], True, False, "bk1", ["KCa%d" % t, "KCb%d" % t, "mON"])
+        MM(T.bk1[:, 0:C], q, tb[:], False, False, "bk1", [("mQT", 128 * t, 128 * t + 128), TB])
+        MM(T.bk1[:, 0:C], q, T.NF[:], False, True, "bk1", [("mQT", 128 * t, 128 * t + 128), "NF"])
+
+    def codesv(t):
+        TB = "TB%d" % t
+        tb = T[TB]
+        tt(T.QF[:], ["QF"], tb[:], T.bk0[:, 0:C], [TB, "bk0"], A.mult)
+        tt(T.FI[:], ["FI"], T.QF[:], T.bk1[:, 0:C], ["QF", "bk1"], A.add)
+        ts(T.XI[:], ["XI"], T.FI[:], ["FI"], 4, 0x7FFF8FFF, SHR, AND)
+
+    def codesw(t):
+        ts(T.OFF[:], ["OFF"], T.XI[:], ["XI"], float(VOID), None, A.min)
+        ts(T.CM[:], ["CM"], T.XI[:], ["XI"], float(VOID - 1), -7.5, A.min, A.add)
+
+    def codes2(t):
+        S(T.MG[:], T.CM[:], ["MG"], ["CM"], scale=1.0 / 16, bias=col(61))
+        S(T.N4[:], T.MG[:], ["N4"], ["MG"], bias=col(62))
+        MM(T.bk6[:, 0:C], T.mFN[:], T.NF[:], True, True, "bk6", ["mFN", "NF"])
+        S(T.FN[:], T.bk6[:, 0:C], ["FN"], ["bk6", ("cF", 10 + t, 11 + t)], F.Relu, scale=col(10 + t))
+
+    codes(0)
+    codesv(0)
+    codesw(0)
+    for i in range(16):
+        if i < 11:
+            S(T.PXP[:, i:W:16], T.P[:], ["PXP%d" % i], ["P"], F.Copy)
+        else:
+            V("cp", T.PXP[:, i:W:16], ["PXP%d" % i], ["P"], T.P[:])
+    allpx = ["PXP%d" % i for i in range(16)]
+
+    eqm("mI16", 0, 0, 16)
+    eqm("mP256", 0, 0, -256)
+    ts(T.cJ[:], ["cJ"], T.cM[:], ["cM"], 15, None, AND)
+    ts(T.mCH[:], ["mCH"], T.cJ[:], ["cJ"], -1.0 / 128, 15.0 / 128, A.mult, A.add)
+
+    def constants():
+        ts(T.cB[:], ["cB"], T.cJ[:], ["cJ"], 1.0, None, A.mult)
+        tt(T.cMI[:], ["cMI"], T.cB[:], T.cA[:], ["cB", "cA"], A.add)
+        for i in range(16):
+            ts(T.mE[:, 128 * i:128 * i + 128], [("mE", 128 * i, 128 * i + 128)], T.cMI[:], ["cMI"], float(i), 4096.0, A.is_equal, A.mult)
+        ts(T.mCV[:], ["mCV"], T.cJ[:], ["cJ"], -2.0, 30.0, A.mult, A.add)
+        V("ms", T.cMASK[:], ["cMASK"], [], 1.0)
+        V("ms", T.cMASK[:, E16(0)], ["cMASK"], [], 0.0)
+        V("ms", T.cNEG[:], ["cNEG"], [], 0.0)
+        V("ms", T.cNEG[:, E16(0)], ["cNEG"], [], -2.0 ** 26)
+        V("cp", T.cBL[:], ["cBL"], ["cG"], T.cG[:])
+        V("cp", T.THF[0:8, :], ["THF"], ["THI"], T.THI[0:8, :])
+        ts(T.KV[0:8, :], ["KV"], T.cG[0:8, :], ["cG"], 1, None, AND)
+        ts(T.TH8[0:8, :], ["TH8"], T.KV[0:8, :], ["KV", "cF", "THF"], T.cF[0:8, 3:4], T.THF[0:8, :], A.is_equal, A.mult)
+        ts(T.cJ[:], ["cJ"], T.cM[:], ["cM"], 5, None, SHR)
+        ts(T.mTH[0:8, :], ["mTH"], T.cJ[0:8, :], ["cJ", "cF"], T.cF[0:8, 5:6], 16.0, A.is_equal, A.mult)
+        MM(T.bk6[:, 0:16], T.mTH[0:8, :], T.TH8[0:8, :], True, True, "bk6", ["mTH", "TH8"])
+        V("cp", T.TH16[:], ["TH16"], ["bk6"], T.bk6[:, 0:16])
+        V("cp", T.LIM[:], ["LIM"], ["bk6"], T.bk6[:, 0:16])
+        ts(T.cB[:], ["cB"], T.cD[:], ["cD"], 256.0, -1.0, A.is_gt, A.mult)
+        tt(T.cB[:], ["cB"], T.cB[:], T.cBM[:], ["cB", "cBM"], A.mult)
+        tt(T.mFN[:], ["mFN"], T.cB[:], T.mI[:], ["cB", "mI"], A.add)
+        fcol(10, 1, float(RHO[0]), 1.0 / FLAG, A.not_equal, A.mult)
+
+    def constants2():
+        S(T.mEX[:], T.mE[:], ["mEX"], ["mE"], F.Copy, scale=16.0)
+        V("ms", T.EA[:], EAS, [], 0.0)
+        V("ms", T.EA[:, E16(4)], ["EA4"], [], 1.0)
+        fcol(20, 1, 1.0, -32.0 / 4096, A.is_equal, A.mult)
+        for r, c in ((2, 2.0), (3, 32.0), (4, 480.0)):
+            fcol(21, 1, float(r), c / 4096, A.is_equal, A.mult)
+            tt(col(20), [("cF", 20, 21)], col(20), col(21), [("cF", 20, 22)], A.add)
+        fcol(22, 1, 0.0, None, A.is_equal)
+        ts(T.mB0[:], ["mB0"], T.cBM[:], ["cBM", ("cF", 22, 23)], col(22), None, A.mult)
+        const_r(0)
+        V("cp", T.mIF[:], ["mIF"], ["mI"], T.mI[:])
+        ts(T.mCX[0:64, :], ["mCX0"], T.mCV[0:64, :], ["mCV"], 32.0, None, A.mult)
+        V("ms", T.mCX[64:128, :], ["mCX1"], [], 15.0 / 128)
+
+    def constants3():
+        ts(T.cDUM[:], ["cDUM"], T.cG[:], ["cG", ("cF", 1, 2)], 16.0, col(1), A.mult, A.add)
+        ts(T.cDUM[:], ["cDUM"], T.cDUM[:], ["cDUM"], float(DUMMY), None, A.add)
+        fcol(23, 2, 0.0, None, A.is_equal)
+        V("ms", T.EB[:], ["EB"], [], 1.0)
+        ts(T.X1[:], ["X1"], T.cG[:], ["cG"], 1, None, SHR)
+        ts(T.KV[:, 0:1], ["KV"], T.cP[:], ["cP"], 31, None, AND)
+        V("cp", col(24), [("cF", 24, 25)], ["KV"], T.KV[:, 0:1])
+        ts(T.EB[:, E16(6)], ["EB"], T.X1[:], ["X1", ("cF", 24, 25)], 32.0, col(24), A.mult, A.add)
+        fcol(25, 1, 3.0, 512.0, A.is_lt, A.mult)
+        fcol(26, 1, 3.0, -256.0, A.is_ge, A.mult)
+        fcol(27, 1, 6.0, 255.0, A.is_ge, A.mult)
+        fcol(28, 1, 7.0, -16383.0, A.is_ge, A.mult)
+        fcol(29, 1, 8.0, 16384.0, A.is_ge, A.mult)
+        for k in (27, 28, 29):
+            tt(col(26), [("cF", 26, 27)], col(26), col(k), [("cF", 26, 30)], A.add)
+        fcol(30, 1, 8.0, -256.0, A.is_ge, A.mult)
+        fcol(31, 1, 11.0, 257.0, A.is_ge, A.mult)
+        fcol(32, 1, 12.0, -1.0, A.is_ge, A.mult)
+        for k in (31, 32):
+            tt(col(30), [("cF", 30, 31)], col(30), col(k), [("cF", 30, 33)], A.add)
+        ts(T.mXX[:], ["mXX"], T.cD[:], ["cD", ("cF", 25, 26)], 256.0, col(25), A.is_equal, A.mult)
+        ts(T.cA[:], ["cA"], T.cD[:], ["cD", ("cF", 26, 27)], 261.0, col(26), A.is_equal, A.mult)
+        tt(T.mXX[:], ["mXX"], T.mXX[:], T.cA[:], ["mXX", "cA"], A.add)
+        ts(T.cA[:], ["cA"], T.cD[:], ["cD", ("cF", 30, 31)], 251.0, col(30), A.is_equal, A.mult)
+        tt(T.mXX[:], ["mXX"], T.mXX[:], T.cA[:], ["mXX", "cA"], A.add)
+        ts(col(33), [("cF", 33, 34)], col(3), ["cF"], 16.0, col(4), A.mult, A.add)
+        for s in range(4):
+            fcol(40 + s, 6, float(s), None, A.is_equal)
+        for a in range(4):
+            if a:
+                fcol(33 + a, 33, 32.0 * a, None, A.add)
+            ts(T.mLM[:, 128 * a:128 * a + 128], ["mLM"], T.cM[:], ["cM", ("cF", 33 + a, 34 + a)], col(33 + a), 8192.0, A.is_equal, A.mult)
+        for s in range(2):
+            for gm in range(2):
+                k = 2 * s + gm
+                ts(T.mLX[:, 128 * k:128 * k + 128], ["mLX"], T.cD[:], ["cD", "cF"], 256.0 + 16 * (gm - s), col(23 if s == 0 else 2), A.is_equal, A.mult)
+
+    n64 = C // CH
+
+    def votes(k):
+        lo, hi = 1024 * k, 1024 * k + 1024
+        for i in range(16):
+            MM(T.bk3[:, n64 * k:n64 * (k + 1)], T.mE[:, 128 * i:128 * i + 128], T.R[:, lo + i:hi:16], False, False, "bk3", [("mE", 128 * i, 128 * i + 128), ("R", lo, hi)])
+
+    for t in range(RO):
+        first = t == 0
+        TB = "TB%d" % t
+        MM(T.bk2[:, 0:C], T.mCH[:], T.mON[:], True, False, "bk2", ["mCH", "mON"])
+        MM(T.bk2[:, 0:C], T.mP256[:], T.P[:], False, False, "bk2", ["mP256", "P"])
+        for k in range(CH):
+            lo, hi = 1024 * k, 1024 * k + 1024
+            off = T.OFF[:, n64 * k:n64 * (k + 1)]
+            tt(T.M[:, lo:hi], [("M", lo, hi)], T.U[:].indirect(off), T.PXP[:, lo:hi], ["U", ("OFF", n64 * k, n64 * (k + 1))] + allpx, A.max)
+            S(T.R[:, lo:hi], T.U[:].indirect(off), [("R", lo, hi)], ["U", ("OFF", n64 * k, n64 * (k + 1))], F.Copy)
+            if first and k == 0:
+                constants()
+            if first and k == 1:
+                codes2(0)
+            if k == 0 and not first:
+                pass
+            for i in range(16):
+                MM(T.bk2[:, n64 * k:n64 * (k + 1)], T.mI16[:], T.M[:, lo + i:hi:16], False, k == CH - 1 and i == 15, "bk2", ["mI16", ("M", lo, hi)])
+            if k == 0:
+                MM(T.bk3[:, 0:C], T.mCV[:], T.mON[:], True, False, "bk3", ["mCV", "mON"])
+            else:
+                votes(k - 1)
+        votes(CH - 1)
+        MM(T.bk3[:, 0:C], T.mI[:], T.N4[:], False, True, "bk3", ["mI", "N4"])
+        if first:
+            constants2()
+
+        V("tr", T.KT[:], ["KT"], ["bk2"], T.bk2[:, 0:C])
+        V("sc", T.S1[:], ["S1"], ["cMASK", "KT"], T.cMASK[:], T.KT[:], 0.0, A.mult, A.max)
+        l3 = T.EA[:, E16(3)]
+        tt(l3, ["EA3"], T.S1[:, 15:C:16], T.LIM[:], ["S1", "LIM"], A.is_lt)
+        ts(T.LB[:], ["LB"], l3, ["EA3"], BIG, None, A.mult)
+        tt(T.TAU[:], ["TAU"], T.LB[:], T.S1[:, 15:C:16], ["LB", "S1"], A.max)
+        tt(T.WT[:], ["WT"], T.TAU[:].indirect(T.cBL[:]), T.KT[:], ["TAU", "cBL", "KT"], A.is_le)
+        V("tr", T.bk4[:, 0:C], ["bk4"], ["WT"], T.WT[:])
+        ts(T.X1[:], ["X1"], T.TAU[:], ["TAU"], 15, None, AND)
+        ts(T.X2[:], ["X2"], T.TAU[:], ["TAU"], 4, 15, SHR, AND)
+        V("cp", T.EA[:, E16(1)], ["EA1"], ["X1"], T.X1[:])
+        V("cp", T.EA[:, E16(2)], ["EA2"], ["X2"], T.X2[:])
+        V("tr", T.VT[:], ["VT"], ["bk3"], T.bk3[:, 0:C])
+        V("sc", T.S2[:], ["S2"], ["cNEG", "VT"], T.cNEG[:], T.VT[:], 0.0, A.add, A.max)
+        V("cp", T.KV[:], ["KV"], ["S2"], T.S2[:, 15:C:16])
+        ts(T.ZV[:], ["ZV"], T.S2[:, 15:C:16], ["S2"], 0.0, None, A.is_ge)
+        ts(T.NB[:], ["NB"], T.KV[:], ["KV"], 255, None, AND)
+        tt(T.ZV[:], ["ZV"], T.ZV[:], l3, ["ZV", "EA3"], A.mult)
+        ts(T.TK[:], ["TK"], T.NB[:], ["NB"], 2.0, -512.0, A.mult, A.add)
+        tt(T.EA[:, E16(0)], ["EA0"], T.TK[:], T.ZV[:], ["TK", "ZV"], A.mult)
+        V("tr", T.EN[:], ["EN"], EAS, T.EA[:])
+        MM(T.bk0[:, 0:C], T.mB0[:], T.EN[:], True, True, "bk0", ["mB0", "EN"])
+        MM(T.bk1[:, 0:C], T.mNR[:, 128 * t:128 * t + 128], T[TB][:], True, False, "bk1", [("mNR", 128 * t, 128 * t + 128), TB])
+        MM(T.bk1[:, 0:C], T.mBR[:, 128 * t:128 * t + 128], T.EN[:], False, True, "bk1", [("mBR", 128 * t, 128 * t + 128), "EN"])
+
+        if t < RO - 1:
+            MM(T.bk6[:, 0:16], T.mON[:, 0:128], l3, True, True, "bk6", ["mON", "EA3"])
+            S(T.MJK[:], T.bk6[:, 0:16], ["MJK", "MC"], ["bk6"], scale=16.0, accum_out=T.MC[:])
+            S(T.MA[:], T.MC[:], ["MA"], ["MC", ("cF", 60, 64)], scale=1.0 / 16, bias=col(63))
+            S(T.MQ[:], T.MA[:], ["MQ"], ["MA", ("cF", 60, 64)], scale=1.0 / 256, bias=col(61))
+            S(T.MR[:], T.MQ[:], ["MR"], ["MQ", ("cF", 60, 64)], bias=col(62))
+            S(T.MF[:], T.MR[:], ["MF"], ["MR", "MC"], scale=-4096.0, bias=T.MC[:])
+
+        MM(T.bk5[:, 0:C], T.mIF[:], T.CM[:], True, False, "bk5", ["mIF", "CM"])
+        MM(T.bk5[:, 0:C], T.mCX[:], T.mON[:], False, False, "bk5", ["mCX0", "mCX1", "mON"])
+
+        def pick(i):
+            tt(T.PR[:, i:W:16], ["PR%d" % i], T.R[:, i:W:16], T.bk4[:, 0:C], ["R", "bk4"], A.mult)
+            MM(T.bk5[:, 0:C], T.mEX[:, 128 * i:128 * i + 128], T.PR[:, i:W:16], False, i == 15, "bk5", ["mEX", "PR%d" % i])
+        for i in range(4):
+            pick(i)
+        a, b = C * t, C * t + C
+        tt(T.DL[:], ["DL"], T.FN[:], T.bk0[:, 0:C], ["FN", "bk0"], A.mult)
+        tt(T.TS[:, a:b], [("TS", a, b)], T.DL[:], T.bk1[:, 0:C], ["DL", "bk1"], A.add)
+        dst = T.cores[(rank + 1) % N] if t < RO - 1 else T.cores[(rank - (RO - 1)) % N]
+        rid, pid, _se = topo.addr(dst)
+        mask = topo.mask(core, dst)
+        src = T.cores[(rank - 1) % N] if t < RO - 1 else T.cores[(rank + RO - 1) % N]
+        order("g", [("TS", a, b)], [], "snd", 0)
+        g.remote_dma(T["TB%d" % (t + 1)][:], T.TS[:, a:b], T.sem["arr%d" % (t + 1)], T.sem["snd"], pid, rid, mask)
+        arrive("TB%d" % (t + 1), "arr%d" % (t + 1), len(topo.engines(src, core)))
+        for i in range(4, 16):
+            pick(i)
+        S(T.W1[:], T.bk4[:, 0:C], ["W1"], ["bk4"], scale=-1.0, bias=1.0)
+        if first:
+            constants3()
+        if t < RO - 1:
+            ts(T.LIM[:], ["LIM"], T.TH16[:], ["TH16", "MF"], T.MF[:], None, A.add)
+
+        V("tr", T.XT[:], ["XT"], ["bk5"], T.bk5[:, 0:C])
+        V("sc", T.S3[:], ["S3"], ["cNEG", "XT"], T.cNEG[:], T.XT[:], 0.0, A.add, A.max)
+        V("cp", T.KI[:], ["KI"], ["S3"], T.S3[:, 15:C:16])
+        ts(T.ZK[:], ["ZK"], T.S3[:, 15:C:16], ["S3"], 0.0, None, A.is_lt)
+        for r in range(3):
+            ts(T["D%d" % r][:], ["D%d" % r], T.KI[:], ["KI"], 4 * r, 15, SHR, AND)
+        tt(T.ZZ[:], ["ZZ"], T.ZK[:], l3, ["ZK", "EA3"], A.max)
+        for r in range(3):
+            V("cp", T.EB[:, E16(r)], ["EBd%d" % r], ["EB", "D%d" % r], T["D%d" % r][:])
+            S(T.EB[:, E16(3 + r)], T.EB[:, E16(r)], ["EBs%d" % r], ["EB", "EBd%d" % r], F.Square)
+        V("cp", T.EB[:, E16(7)], ["EBz"], ["EB", "ZZ"], T.ZZ[:])
+        ts(T.XC[:], ["XC"], T.KI[:], ["KI"], 4095, None, AND)
+        ts(T.ZK[:], ["ZK"], T.ZZ[:], ["ZZ"], 8192.0, None, A.mult)
+        tt(T.XF[:], ["XF"], T.XC[:], T.ZK[:], ["XC", "ZK"], A.add)
+        V("tr", T.VN[:], ["VN"], ["EB", "EBz"] + ["EBd%d" % r for r in range(3)] + ["EBs%d" % r for r in range(3)], T.EB[:])
+        MM(T.bk7[:, 0:C], T.mXX[:], T.VN[:], True, True, "bk7", ["mXX", "VN"])
+        ts(T.VM[:, 0:2 * C:2], ["VM0"], T.VN[:], ["VN", ("cF", 23, 24)], col(23), None, A.mult)
+        ts(T.VM[:, 1:2 * C:2], ["VM1"], T.VN[:], ["VN", ("cF", 2, 3)], col(2), None, A.mult)
+        S(T.RV[:], T.bk7[:, 0:C], ["RV"], ["bk7"], F.Copy)
+        if t < RO - 1:
+            if first:
+                const_t(1)
+            codes(t + 1)
+            const_r(t + 1)
+            if t + 2 < RO:
+                const_t(t + 2)
+        banks = ["bk2", "bk3", "bk4", "bk5", "bk7"]
+        use = [0]
+
+        def block(a, be):
+            bank = banks[use[0] % len(banks)]
+            use[0] += 1
+            n = 64 * (be + 1)
+            MM(T[bank][:, 0:n], T.VM[32 * a:32 * a + 32, 128 * be:128 * be + 128], T.RV[32 * a:32 * a + 32, 0:n], True, True, bank, ["VM0", "VM1", "RV"])
+            k = 4 * a + be
+            if (a, be) in S_RED:
+                S(T.JK[:, 0:n], T[bank][:, 0:n], ["JK", ("FL", k, k + 1)], [bank], F.Relu, accum_out=T.FL[:, k:k + 1])
+            else:
+                V("rd", T.FL[:, k:k + 1], [("FL", k, k + 1)], [bank], T[bank][:, 0:n], AxisListType.X, A.max)
+        for be in (3, 2, 1, 0):
+            for a in range(4):
+                block(a, be)
+        for s in range(2):
+            for gm in range(2):
+                k = 2 * s + gm
+                MM(T.bk6[:, s:16:2], T.mLX[:, 128 * k:128 * k + 128], T.XF[:, gm:16:2], gm == 0, gm == 1, "bk6", ["mLX", "XF"])
+        tt(T.XL[:], ["XL"], T.cDUM[:], T.bk6[:, 0:16], ["cDUM", "bk6"], A.min)
+        for s in range(4):
+            ts(T.FB[:, s:64:4], ["FB%d" % s], T.FL[:], ["FL", ("cF", 40 + s, 41 + s)], 0.0, col(40 + s), A.is_gt, A.mult)
+        for a in range(4):
+            MM(T.bk7[:, 0:16], T.mLM[:, 128 * a:128 * a + 128], T.FB[:, 16 * a:16 * a + 16], a == 0, a == 3, "bk7", ["mLM"] + ["FB%d" % s for s in range(4)])
+        if t < RO - 1:
+            codesv(t + 1)
+        tt(T.YL[:], ["YL"], T.XL[:], T.bk7[:, 0:16], ["XL", "bk7"], A.add)
+        tt(T.YM[:], ["YM"], T.YL[:], T.cDUM[:], ["YL", "cDUM"], A.min)
+        V("cp", T.OL[:], ["OL"], ["YM"], T.YM[:])
+        S(T.UG[:], T.U[:].indirect(T.OL[:]), ["UG"], ["U", "OL"], F.Copy)
+        if t < RO - 1:
+            codesw(t + 1)
+            codes2(t + 1)
+        tt(T.U[:].indirect(T.OL[:]), ["U"], T.UG[:], T.W1[:], ["UG", "W1", "OL"], A.mult)
+
+    S(T.OUTT[:], T["TB%d" % RO][:], ["OUTT"], ["TB%d" % RO], scale=0.5)
+    dma("s", 4, T.yt[:], T.OUTT[:], ["OUTT"], ["yt"])
+    for i in range(16):
+        MM(T.bk0[:, 0:C], T.mI[:], T.U[:, i:W:16], i == 0, i == 15, "bk0", ["mI", "U"])
+    V("cp", T.OUTC[:], ["OUTC"], ["bk0"], T.bk0[:, 0:C])
+    dma("y", 5, T.yc[:], T.OUTC[:], ["OUTC"], ["yc"])
+    need("y", "dma4", 16)
+    need("y", "dma5", 16)
+    g.wait_ge(T.sem["snd"], sum(len(topo.engines(core, T.cores[(rank + 1) % N] if t < RO - 1 else T.cores[(rank - (RO - 1)) % N])) for t in range(RO)))

@@ -8,8 +8,10 @@ UW = 4368
 VOID = 4096
 DUMMY = 4112
 FLAG = 2.0 ** 19
-BIG = 2.0 ** 20
+BIG = 2.0 ** 25
+MAGIC = 1.5 * 2.0 ** 23
 CH = 4
+NT = C // CH
 S_RED = [(a, b) for a in range(4) for b in range(4) if b != 1 and (a, b) not in ((3, 3), (3, 0))]
 RHO = [(5 * t) % 16 for t in range(RO)]
 
@@ -20,28 +22,29 @@ for _n, _w, _d in [
     ("FI", C, "int32"), ("XI", C, "int32"), ("OFF", C, "uint16"), ("CM", C, "float32"), ("MG", C, "float32"), ("N4", C, "bfloat16"),
     ("KT", C, "float32"), ("S1", C, "float32"), ("VT", C, "float32"), ("S2", C, "float32"), ("XT", C, "float32"), ("S3", C, "float32"),
     ("WT", C, "float32"), ("W1", C, "bfloat16"), ("EA", C, "bfloat16"), ("EN", C, "bfloat16"), ("EB", C, "bfloat16"), ("VN", C, "bfloat16"),
-    ("VM", 2 * C, "bfloat16"), ("RV", C, "bfloat16"), ("JK", C, "bfloat16"), ("DL", C, "bfloat16"), ("NV", C, "bfloat16"),
-    ("TAU", 16, "int32"), ("LB", 16, "float32"), ("KV", 16, "int32"), ("NB", 16, "int32"), ("TK", 16, "float32"), ("ZV", 16, "float32"),
+    ("VM", 2 * C, "bfloat16"), ("RV", C, "bfloat16"), ("JK", C, "bfloat16"), ("DL", C, "bfloat16"), ("UG", C, "bfloat16"),
+    ("TAU", 16, "int32"), ("LB", 16, "float32"), ("TV", 16, "float32"), ("KV", 16, "int32"), ("NB", 16, "int32"),
     ("X1", 16, "int32"), ("X2", 16, "int32"), ("KI", 16, "int32"), ("D0", 16, "int32"), ("D1", 16, "int32"), ("D2", 16, "int32"),
-    ("ZK", 16, "float32"), ("ZZ", 16, "float32"), ("XC", 16, "int32"), ("XF", 16, "float32"), ("XL", 16, "float32"), ("YL", 16, "float32"), ("YM", 16, "float32"),
-    ("OL", 16, "uint16"), ("FL", 16, "float32"), ("FB", 64, "bfloat16"), ("LIM", 16, "float32"), ("TH16", 16, "float32"), ("THI", 1, "int32"),
-    ("THF", 1, "float32"), ("TH8", 16, "float32"), ("MC", 1, "float32"), ("MA", 1, "float32"), ("MQ", 1, "float32"), ("MR", 1, "float32"), ("MF", 1, "float32"), ("MJK", 16, "float32"), ("UG", C, "bfloat16"),
-    ("OUTT", C, "float32"), ("OUTC", C, "float32"),
-    ("cM", 128, "int32"), ("cD", 128, "int32"), ("cJ", 128, "int32"), ("cT", 128, "int32"), ("cG", 16, "int32"), ("cH", 16, "int32"),
-    ("cP", 1, "int32"), ("cI", 8, "int32"), ("cF", 64, "float32"), ("cBM", 128, "bfloat16"), ("cMI", 128, "bfloat16"), ("cDD", 128, "bfloat16"), ("cDM", 128, "bfloat16"),
+    ("YM", 16, "float32"), ("OL", 16, "uint16"), ("FL", 16, "float32"), ("FB", 64, "bfloat16"),
+    ("LIM", 16, "float32"), ("TH16", 16, "float32"), ("THI", 1, "int32"), ("THF", 1, "float32"), ("TH8", 16, "float32"), ("THQ", 16, "int32"),
+    ("MC", 1, "float32"), ("MA", 1, "float32"), ("MQ", 1, "float32"), ("MR", 1, "float32"), ("MF", 1, "float32"), ("MJK", 16, "float32"),
+    ("OUTT", C, "float32"), ("OUTC", C, "float32"), ("TS", C * RO, "bfloat16"),
+    ("cM", 128, "int32"), ("cD", 128, "int32"), ("cJ", 128, "int32"), ("cT", 128, "int32"), ("cG", 16, "int32"),
+    ("cP", 1, "int32"), ("cI", 8, "int32"), ("cF", 64, "float32"), ("cBM", 128, "bfloat16"), ("cMI", 128, "bfloat16"), ("cDD", 128, "bfloat16"),
     ("cA", 128, "bfloat16"), ("cB", 128, "bfloat16"), ("mI", 128, "bfloat16"), ("mI16", 128, "bfloat16"), ("mP256", 128, "bfloat16"), ("mIF", 128, "float32"),
     ("mPT", 128 * RO, "bfloat16"), ("mQT", 128 * RO, "bfloat16"), ("mKC", 128 * RO, "bfloat16"), ("iKC", 128 * RO, "int32"), ("jKC", 128 * RO, "int32"),
-    ("mE", 2048, "bfloat16"), ("mEX", 2048, "bfloat16"), ("mCH", 128, "bfloat16"), ("mCV", 128, "bfloat16"), ("mCX", 128, "bfloat16"),
-    ("mFN", 128, "bfloat16"), ("mBR", 128 * RO, "bfloat16"), ("mNR", 128 * RO, "bfloat16"), ("mB0", 128, "bfloat16"), ("mON", C, "bfloat16"),
-    ("mXX", 128, "bfloat16"), ("mLM", 512, "bfloat16"), ("mLX", 512, "float32"), ("mTH", 128, "float32"),
-    ("cMASK", C, "float32"), ("cNEG", C, "float32"), ("cBL", 16, "uint16"), ("cDUM", 16, "float32"), ("TS", C * RO, "bfloat16"),
+    ("mE", 2048, "bfloat16"), ("mEX", 2048, "bfloat16"), ("mEL", 2048, "bfloat16"), ("mCH", 128, "bfloat16"), ("mCV", 128, "bfloat16"), ("mCX", 128, "bfloat16"),
+    ("mF0", 128, "bfloat16"), ("mFN", 128 * RO, "bfloat16"), ("mBR", 128 * RO, "bfloat16"), ("mNR", 128 * RO, "bfloat16"), ("mB0", 128, "bfloat16"), ("mON", C, "bfloat16"),
+    ("mXX", 128, "bfloat16"), ("mZ", 128, "bfloat16"), ("mLM", 512, "bfloat16"), ("mTH", 128, "float32"),
+    ("cMASK", C, "float32"), ("cNEG", C, "float32"), ("cBL", 16, "uint16"), ("cDUM", 16, "float32"),
 ]:
     SCRATCH[_n] = ("sbuf", [128, _w], _d)
 for _t in range(RO + 1):
     SCRATCH["TB%d" % _t] = ("sbuf", [128, C], "bfloat16")
 for _b in range(8):
     SCRATCH["bk%d" % _b] = ("psum", [128, 512], "float32")
-SEMAPHORES = ["v", "s", "p", "g", "snd"] + ["arr%d" % t for t in range(1, RO + 1)] + ["dma%d" % k for k in range(8)]
+SEMAPHORES = ["v", "s", "p", "g", "snd"] + ["arr%d" % t for t in range(1, RO + 1)] + ["dma%d" % k for k in range(6)]
+AND, SHR = A.bitwise_and, A.arith_shift_right
 
 
 def rank_program(g, core, T, topo):
@@ -64,21 +67,15 @@ def rank_program(g, core, T, topo):
                 known[q][k] = x
 
     def spans(views):
-        out = []
-        for x in views:
-            if isinstance(x, str):
-                x = (x, 0, 1 << 20)
-            out.append(x)
-        return out
+        return [(x, 0, 1 << 20) if isinstance(x, str) else x for x in views]
 
-    def order(q, reads, writes, sem, val):
+    def order(q, reads, writes):
         todo = {}
         reads, writes = spans(reads), spans(writes)
         for views, wr in ((reads, False), (writes, True)):
             for b, lo, hi in views:
-                bank = b.startswith("bk")
                 for l2, h2, w2, q2, s2, v2 in last.get(b, []):
-                    if bank:
+                    if b.startswith("bk"):
                         hit = q2 != q or (w2 and q != "p")
                     else:
                         hit = (wr or w2) and l2 < hi and lo < h2
@@ -91,13 +88,10 @@ def rank_program(g, core, T, topo):
     def note(q, reads, writes, sem, val):
         for views, wr in ((reads, False), (writes, True)):
             for b, lo, hi in views:
-                bank = b.startswith("bk")
                 keep = []
                 for e in last.get(b, []):
-                    if bank:
-                        if e[3] == q and (wr or not e[2]):
-                            continue
-                        if e[3] != q:
+                    if b.startswith("bk"):
+                        if e[3] != q or wr or not e[2]:
                             continue
                     elif wr and lo <= e[0] and e[1] <= hi:
                         continue
@@ -111,20 +105,16 @@ def rank_program(g, core, T, topo):
         done[(sem, val)] = know
 
     def run(q, call, reads, writes):
-        val = count.get(q, 0) + 1
-        reads, writes = order(q, reads, writes, q, val)
+        reads, writes = order(q, reads, writes)
         call(queue[q]).then_inc(T.sem[q], 1)
-        count[q] = val
-        note(q, reads, writes, q, val)
+        count[q] = count.get(q, 0) + 1
+        note(q, reads, writes, q, count[q])
 
     def dma(q, k, out, in_, reads, writes):
         sem = "dma%d" % k
-        reads, writes = order(q, reads, writes, sem, 16)
+        reads, writes = order(q, reads, writes)
         queue[q].dma_start(out, in_).then_inc(T.sem[sem], 16)
         note(q, reads, writes, sem, 16)
-
-    def arrive(buf, sem, val):
-        last[buf] = [(0, 1 << 20, True, "r", sem, val)]
 
     def V(name, out, wr, rd, *a, **k):
         run("v", lambda e: {"tt": e.tensor_tensor, "ts": e.tensor_scalar, "cp": e.tensor_copy, "tr": e.transpose, "sc": e.tensor_tensor_scan,
@@ -136,9 +126,6 @@ def rank_program(g, core, T, topo):
     def MM(out, lhsT, rhs, start, stop, bank, rd):
         run("p", lambda e: e.matmul(out, lhsT, rhs, start, stop), rd, [bank])
 
-    def col(k):
-        return T.cF[:, k:k + 1]
-
     def ts(out, wr, in0, rd, s1, s2, op0, op1=None):
         if op1 is None:
             V("ts", out, wr, rd, in0, s1, None, op0)
@@ -148,347 +135,353 @@ def rank_program(g, core, T, topo):
     def tt(out, wr, a, b, rd, op):
         V("tt", out, wr, rd, a, b, op)
 
-    EAS = ["EA%d" % r for r in range(5)]
-    E16 = lambda r: slice(r, C, 16)
+    def iota(out, wr, pattern, base, cm):
+        run("g", lambda e: e.iota(out, pattern, base, cm), [], [wr])
 
-    dma("y", 0, T.TI[:], T.tst[:], [], ["TI"])
-    dma("s", 1, T.P[:], T.pr[:], [], ["P"])
-    dma("s", 2, T.THI[0:8, :], T.th[:], [], ["THI"])
-    dma("y", 3, T.U[:, 0:W], T.cov[:], [], [("U", 0, W)])
+    def fill(name, c0, pattern, base, cm, value, src=None, s0=0):
+        n = 1
+        for p in pattern:
+            n *= p[1]
+        if src is None:
+            src, s0 = name, c0
+        run("g", lambda e: e.affine_select(T[name][:, c0:c0 + n], T[src][:, s0:s0 + n], pattern, A.not_equal, value, base, cm),
+            [(src, s0, s0 + n)], [(name, c0, c0 + n)])
 
-    def iota(name, pattern, base, cm):
-        run("g", lambda e: e.iota(T[name][:], pattern, base, cm), [], [name])
-    iota("cD", [[1, 128]], 256, -1)
-    iota("cM", [[1, 128]], 0, 0)
-    iota("cP", [[0, 1]], 0, 1)
-    iota("iKC", [[77, RO], [0, 8], [613, 16]], 0, 0)
-    iota("cG", [[1, 16]], 0, 0)
+    def cell(name, c0, row, column, value, src=None, s0=0):
+        fill(name, c0, [[-16, 8], [1000, 16]], -row - 1000 * column, 1, value, src, s0)
 
-    V("ms", T.U[:, W:UW], [("U", W, UW)], [], -1.0)
-    V("ms", T.mON[:], ["mON"], [], 1.0)
-    for k, x in ((60, -511.0 * FLAG), (61, 1.5 * 2.0 ** 23), (62, -1.5 * 2.0 ** 23), (63, -127.5)):
-        V("ms", T.cF[:, k:k + 1], [("cF", k, k + 1)], [], x)
-    def sh(name, src, ops, lo=0, hi=128):
-        if len(ops) == 1:
-            ts(name[0][:], [name[1]], src[0][:], [src[1]], ops[0][1], None, ops[0][0])
-        else:
-            ts(name[0][:], [name[1]], src[0][:], [src[1]], ops[0][1], ops[1][1], ops[0][0], ops[1][0])
-    AND, SHR = A.bitwise_and, A.arith_shift_right
-    def icol(k, ops, op2=None):
-        if len(ops) == 1:
-            ts(T.cI[:, k:k + 1], [("cI", k, k + 1)], T.cP[:], ["cP"], ops[0][1], None, ops[0][0])
-        else:
-            ts(T.cI[:, k:k + 1], [("cI", k, k + 1)], T.cP[:], ["cP"], ops[0][1], ops[1][1], ops[0][0], ops[1][0])
-    icol(0, [(SHR, 4)])
-    icol(1, [(AND, 15)])
-    icol(2, [(SHR, 4), (AND, 1)])
-    icol(3, [(AND, 1)])
-    icol(4, [(AND, 31), (SHR, 1)])
-    icol(5, [(SHR, 1)])
-    icol(6, [(SHR, 5)])
-    V("cp", T.cF[:, 0:7], [("cF", 0, 7)], ["cI"], T.cI[:, 0:7])
+    def col(k):
+        return T.cF[:, k:k + 1]
 
     def fcol(k, src, s1, s2, op0, op1=None):
         ts(col(k), [("cF", k, k + 1)], col(src), [("cF", src, src + 1)], s1, s2, op0, op1)
 
+    def icol(k, s1, s2, op0, op1=None):
+        ts(T.cI[:, k:k + 1], [("cI", k, k + 1)], T.cP[:], ["cP"], s1, s2, op0, op1)
+
+    EAS = ["EA%d" % r for r in range(6)]
+    E16 = lambda r: slice(r, C, 16)
+    blk = lambda name, k: (T[name][:, 128 * k:128 * k + 128], (name, 128 * k, 128 * k + 128))
+
+    dma("y", 0, T.TI[:], T.tst[:], [], ["TI"])
+    dma("s", 1, T.P[:], T.pr[:], [], ["P"])
+    dma("y", 3, T.U[:, 0:W], T.cov[:], [], [("U", 0, W)])
+    dma("s", 2, T.THI[0:8, :], T.th[:], [], ["THI"])
+
+    iota(T.cD[:], "cD", [[1, 128]], 256, -1)
+    iota(T.cM[:], "cM", [[1, 128]], 0, 0)
+    iota(T.cP[:], "cP", [[0, 1]], 0, 1)
+    V("ms", T.mON[:], ["mON"], [], 1.0)
+    for k, x in ((60, -511.0 * FLAG), (61, MAGIC), (62, -MAGIC), (63, -127.5), (59, BIG)):
+        V("ms", T.cF[:, k:k + 1], [("cF", k, k + 1)], [], x)
+
+    def icodes(t):
+        iota(blk("iKC", t)[0], blk("iKC", t)[1], [[0, 8], [613, 16]], 77 * t, 0)
+    icodes(0)
+    iota(T.cG[:], "cG", [[1, 16]], 0, 0)
+    icol(0, 4, None, SHR)
+    icol(1, 15, None, AND)
+    icol(2, 4, 1, SHR, AND)
+    icol(3, 1, None, AND)
+    icol(4, 31, 1, AND, SHR)
+    icol(5, 1, None, SHR)
+    icol(6, 5, None, SHR)
+    icol(7, 31, None, AND)
+    V("cp", T.cF[:, 0:8], [("cF", 0, 8)], ["cI"], T.cI[:])
     ts(T.cJ[:], ["cJ"], T.cM[:], ["cM"], 4, None, SHR)
-    ts(T.cBM[:], ["cBM"], T.cJ[:], ["cJ", ("cF", 0, 1)], col(0), None, A.is_equal)
-    ts(T.cA[:], ["cA"], T.cBM[:], ["cBM"], -100.0, 100.0, A.mult, A.add)
     ts(T.cT[:], ["cT"], T.cD[:], ["cD"], 15, None, AND)
+    ts(T.cBM[:], ["cBM"], T.cJ[:], ["cJ", ("cF", 0, 1)], col(0), None, A.is_equal)
     ts(T.cB[:], ["cB"], T.cT[:], ["cT"], 1.0, None, A.mult)
+    ts(T.cA[:], ["cA"], T.cBM[:], ["cBM"], -100.0, 100.0, A.mult, A.add)
     tt(T.cDD[:], ["cDD"], T.cB[:], T.cA[:], ["cA", "cB"], A.add)
-    def eqm(name, c0, val, scale):
-        ts(T[name][:, c0:c0 + 128], [(name, c0, c0 + 128)], T.cDD[:], ["cDD"], float(val), float(scale), A.is_equal, A.mult)
+
+    def eqm(name, k, val, scale):
+        ts(blk(name, k)[0], [blk(name, k)[1]], T.cDD[:], ["cDD"], float(val), float(scale), A.is_equal, A.mult)
     eqm("mI", 0, 0, 1)
 
     def const_t(t):
-        eqm("mPT", 128 * t, (-(1 + t)) % 16, 1)
-        tt(T.mQT[:, 128 * t:128 * t + 128], [("mQT", 128 * t, 128 * t + 128)], T.mPT[:, 128 * t:128 * t + 128], T.mI[:], [("mPT", 128 * t, 128 * t + 128), "mI"], A.add)
+        eqm("mPT", t, (-(1 + t)) % 16, 1)
+        if t == 0:
+            tt(blk("mQT", t)[0], [blk("mQT", t)[1]], blk("mPT", t)[0], T.mI[:], [blk("mPT", t)[1], "mI"], A.add)
         x = slice(128 * t, 128 * t + 128)
         for p0, nm, bits, add in ((0, "KCa%d" % t, 4080, 0.0), (64, "KCb%d" % t, 15, 1.0 / 64)):
-            ts(T.jKC[p0:p0 + 64, x], ["j" + nm], T.iKC[p0:p0 + 64, x], ["iKC"], bits, None, AND)
+            ts(T.jKC[p0:p0 + 64, x], ["j" + nm], T.iKC[p0:p0 + 64, x], [blk("iKC", t)[1]], bits, None, AND)
             ts(T.mKC[p0:p0 + 64, x], [nm], T.jKC[p0:p0 + 64, x], ["j" + nm], 0.25, add, A.mult, A.add)
 
-    def const_r(t):
+    def const_g(t):
         rho = RHO[t]
         if t:
-            fcol(10 + t, 1, float(rho), 1.0 / FLAG, A.not_equal, A.mult)
-        ts(T.mBR[:, 128 * t:128 * t + 128], [("mBR", 128 * t, 128 * t + 128)], T.mE[:, 128 * rho:128 * rho + 128], [("mE", 128 * rho, 128 * rho + 128), ("cF", 20, 21)], col(20), None, A.mult)
-        ts(T.mNR[:, 128 * t:128 * t + 128], [("mNR", 128 * t, 128 * t + 128)], T.mI[:], ["mI", ("cF", 10 + t, 11 + t)], col(10 + t), FLAG, A.mult, A.mult)
+            fill("mQT", 128 * t, [[-1, 128]], 0, 1, 1.0, "mPT", 128 * t)
+        fill("mFN", 128 * t, [[0, 8], [1, 16]], -rho, 0, 0.0, "mF0", 0)
+        cell("mNR", 128 * t, rho, rho, 0.0, "mI", 0)
+        for k, (r, x) in enumerate(((1, -32.0), (2, 2.0), (3, 32.0), (4, 480.0))):
+            if k == 0:
+                cell("mBR", 128 * t, r, rho, x, "mZ", 0)
+            else:
+                cell("mBR", 128 * t, r, rho, x)
     const_t(0)
     ts(T.TB0[:], ["TB0"], T.TI[:], ["TI"], 2.0, None, A.mult)
 
     def codes(t):
         TB = "TB%d" % t
         tb = T[TB]
-        S(T.NF[:], tb[:], ["NF"], [TB, ("cF", 60, 63)], F.Relu, scale=FLAG, bias=col(60))
-        MM(T.bk0[:, 0:C], T.mPT[:, 128 * t:128 * t + 128], tb[:], True, True, "bk0", [("mPT", 128 * t, 128 * t + 128), TB])
-        q = T.mQT[:, 128 * t:128 * t + 128]
-        MM(T.bk1[:, 0:C], T.mKC[:, 128 * t:128 * t + 128], T.mON[:], True, False, "bk1", ["KCa%d" % t, "KCb%d" % t, "mON"])
-        MM(T.bk1[:, 0:C], q, tb[:], False, False, "bk1", [("mQT", 128 * t, 128 * t + 128), TB])
-        MM(T.bk1[:, 0:C], q, T.NF[:], False, True, "bk1", [("mQT", 128 * t, 128 * t + 128), "NF"])
+        S(T.NF[:], tb[:], ["NF"], [TB, ("cF", 59, 64)], F.Relu, scale=FLAG, bias=col(60))
+        MM(T.bk0[:, 0:C], blk("mPT", t)[0], tb[:], True, True, "bk0", [blk("mPT", t)[1], TB])
+        MM(T.bk1[:, 0:C], blk("mKC", t)[0], T.mON[:], True, False, "bk1", ["KCa%d" % t, "KCb%d" % t, "mON"])
+        MM(T.bk1[:, 0:C], blk("mQT", t)[0], tb[:], False, False, "bk1", [blk("mQT", t)[1], TB])
+        MM(T.bk1[:, 0:C], blk("mQT", t)[0], T.NF[:], False, True, "bk1", [blk("mQT", t)[1], "NF"])
 
-    def codesv(t):
-        TB = "TB%d" % t
-        tb = T[TB]
-        tt(T.QF[:], ["QF"], tb[:], T.bk0[:, 0:C], [TB, "bk0"], A.mult)
-        tt(T.FI[:], ["FI"], T.QF[:], T.bk1[:, 0:C], ["QF", "bk1"], A.add)
-        ts(T.XI[:], ["XI"], T.FI[:], ["FI"], 4, 0x7FFF8FFF, SHR, AND)
-
-    def codesw(t):
-        ts(T.OFF[:], ["OFF"], T.XI[:], ["XI"], float(VOID), None, A.min)
-        ts(T.CM[:], ["CM"], T.XI[:], ["XI"], float(VOID - 1), -7.5, A.min, A.add)
+    def codev(t, k):
+        if k == 0:
+            tt(T.QF[:], ["QF"], T["TB%d" % t][:], T.bk0[:, 0:C], ["TB%d" % t, "bk0"], A.mult)
+        elif k == 1:
+            tt(T.FI[:], ["FI"], T.QF[:], T.bk1[:, 0:C], ["QF", "bk1"], A.add)
+        elif k == 2:
+            ts(T.XI[:], ["XI"], T.FI[:], ["FI"], 4, 0x7FFF8FFF, SHR, AND)
+        elif k == 3:
+            ts(T.OFF[:], ["OFF"], T.XI[:], ["XI"], float(VOID), None, A.min)
+        else:
+            ts(T.CM[:], ["CM"], T.XI[:], ["XI"], float(VOID - 1), -7.5, A.min, A.add)
 
     def codes2(t):
-        S(T.MG[:], T.CM[:], ["MG"], ["CM"], scale=1.0 / 16, bias=col(61))
-        S(T.N4[:], T.MG[:], ["N4"], ["MG"], bias=col(62))
-        MM(T.bk6[:, 0:C], T.mFN[:], T.NF[:], True, True, "bk6", ["mFN", "NF"])
-        S(T.FN[:], T.bk6[:, 0:C], ["FN"], ["bk6", ("cF", 10 + t, 11 + t)], F.Relu, scale=col(10 + t))
+        S(T.MG[:], T.CM[:], ["MG"], ["CM", ("cF", 59, 64)], scale=1.0 / 16, bias=col(61))
+        S(T.N4[:], T.MG[:], ["N4"], ["MG", ("cF", 59, 64)], bias=col(62))
+        MM(T.bk6[:, 0:C], blk("mFN", t)[0], T.NF[:], True, True, "bk6", [blk("mFN", t)[1], "NF"])
+        S(T.FN[:], T.bk6[:, 0:C], ["FN"], ["bk6"], F.Relu, scale=1.0 / FLAG)
 
     codes(0)
-    codesv(0)
-    codesw(0)
+    for k in range(5):
+        codev(0, k)
+    allpx = ["PXP%d" % i for i in range(16)]
     for i in range(16):
         if i < 11:
-            S(T.PXP[:, i:W:16], T.P[:], ["PXP%d" % i], ["P"], F.Copy)
+            S(T.PXP[:, i:W:16], T.P[:], [allpx[i]], ["P"], F.Copy)
         else:
-            V("cp", T.PXP[:, i:W:16], ["PXP%d" % i], ["P"], T.P[:])
-    allpx = ["PXP%d" % i for i in range(16)]
+            V("cp", T.PXP[:, i:W:16], [allpx[i]], ["P"], T.P[:])
+    V("ms", T.U[:, W:UW], [("U", W, UW)], [], -1.0)
 
-    eqm("mI16", 0, 0, 16)
-    eqm("mP256", 0, 0, -256)
+    S(T.mI16[:], T.mI[:], ["mI16"], ["mI"], F.Copy, scale=16.0)
+    S(T.mP256[:], T.mI[:], ["mP256"], ["mI"], F.Copy, scale=-256.0)
     ts(T.cJ[:], ["cJ"], T.cM[:], ["cM"], 15, None, AND)
     ts(T.mCH[:], ["mCH"], T.cJ[:], ["cJ"], -1.0 / 128, 15.0 / 128, A.mult, A.add)
+    ts(T.cB[:], ["cB"], T.cJ[:], ["cJ"], 1.0, None, A.mult)
+    ts(T.mCV[:], ["mCV"], T.cJ[:], ["cJ"], -2.0, 30.0, A.mult, A.add)
+    tt(T.cMI[:], ["cMI"], T.cB[:], T.cA[:], ["cB", "cA"], A.add)
+    ts(T.cB[:], ["cB"], T.cD[:], ["cD"], 256.0, -1.0, A.is_gt, A.mult)
+    V("ms", T.mZ[:], ["mZ"], [], 0.0)
+    tt(T.cB[:], ["cB"], T.cB[:], T.cBM[:], ["cB", "cBM"], A.mult)
+    V("ms", T.mXX[:], ["mXX"], [], 0.0)
+    tt(T.mF0[:], ["mF0"], T.cB[:], T.mI[:], ["cB", "mI"], A.add)
+    for i in range(16):
+        ts(blk("mE", i)[0], [blk("mE", i)[1]], T.cMI[:], ["cMI"], float(i), 4096.0, A.is_equal, A.mult)
+    const_g(0)
+    fill("mB0", 0, [[-16, 8], [0, 16]], 0, 1, 2.0, "mZ", 0)
+    fill("mB0", 0, [[-16, 8], [0, 16]], -5, 1, -512.0)
+    for r, m, x in [(k, k, 512.0) for k in range(3)] + [(3 + k, 8 + k, -256.0) for k in range(3)] + [(8 + k, 3 + k, -256.0) for k in range(3)] + \
+            [(6, 11, -1.0), (11, 6, 1.0), (7, 12, -16384.0)]:
+        cell("mXX", 0, r, m, x)
+    S(T.mIF[:], T.mI[:], ["mIF"], ["mI"], F.Copy)
 
-    def constants():
-        ts(T.cB[:], ["cB"], T.cJ[:], ["cJ"], 1.0, None, A.mult)
-        tt(T.cMI[:], ["cMI"], T.cB[:], T.cA[:], ["cB", "cA"], A.add)
-        for i in range(16):
-            ts(T.mE[:, 128 * i:128 * i + 128], [("mE", 128 * i, 128 * i + 128)], T.cMI[:], ["cMI"], float(i), 4096.0, A.is_equal, A.mult)
-        ts(T.mCV[:], ["mCV"], T.cJ[:], ["cJ"], -2.0, 30.0, A.mult, A.add)
+    def constants_a():
         V("ms", T.cMASK[:], ["cMASK"], [], 1.0)
-        V("ms", T.cMASK[:, E16(0)], ["cMASK"], [], 0.0)
         V("ms", T.cNEG[:], ["cNEG"], [], 0.0)
+        V("ms", T.cMASK[:, E16(0)], ["cMASK"], [], 0.0)
         V("ms", T.cNEG[:, E16(0)], ["cNEG"], [], -2.0 ** 26)
         V("cp", T.cBL[:], ["cBL"], ["cG"], T.cG[:])
         V("cp", T.THF[0:8, :], ["THF"], ["THI"], T.THI[0:8, :])
-        ts(T.KV[0:8, :], ["KV"], T.cG[0:8, :], ["cG"], 1, None, AND)
-        ts(T.TH8[0:8, :], ["TH8"], T.KV[0:8, :], ["KV", "cF", "THF"], T.cF[0:8, 3:4], T.THF[0:8, :], A.is_equal, A.mult)
+        ts(T.THQ[0:8, :], ["THQ"], T.cG[0:8, :], ["cG"], 1, None, AND)
         ts(T.cJ[:], ["cJ"], T.cM[:], ["cM"], 5, None, SHR)
-        ts(T.mTH[0:8, :], ["mTH"], T.cJ[0:8, :], ["cJ", "cF"], T.cF[0:8, 5:6], 16.0, A.is_equal, A.mult)
+        ts(T.TH8[0:8, :], ["TH8"], T.THQ[0:8, :], ["THQ", ("cF", 0, 8), "THF"], T.cF[0:8, 3:4], T.THF[0:8, :], A.is_equal, A.mult)
+        ts(T.mTH[0:8, :], ["mTH"], T.cJ[0:8, :], ["cJ", ("cF", 0, 8)], T.cF[0:8, 5:6], 16.0, A.is_equal, A.mult)
+        V("ms", T.EA[:], EAS, [], 0.0)
+        V("ms", T.EA[:, E16(4)], ["EA4"], [], 1.0)
         MM(T.bk6[:, 0:16], T.mTH[0:8, :], T.TH8[0:8, :], True, True, "bk6", ["mTH", "TH8"])
         V("cp", T.TH16[:], ["TH16"], ["bk6"], T.bk6[:, 0:16])
         V("cp", T.LIM[:], ["LIM"], ["bk6"], T.bk6[:, 0:16])
-        ts(T.cB[:], ["cB"], T.cD[:], ["cD"], 256.0, -1.0, A.is_gt, A.mult)
-        tt(T.cB[:], ["cB"], T.cB[:], T.cBM[:], ["cB", "cBM"], A.mult)
-        tt(T.mFN[:], ["mFN"], T.cB[:], T.mI[:], ["cB", "mI"], A.add)
-        fcol(10, 1, float(RHO[0]), 1.0 / FLAG, A.not_equal, A.mult)
-
-    def constants2():
-        S(T.mEX[:], T.mE[:], ["mEX"], ["mE"], F.Copy, scale=16.0)
-        V("ms", T.EA[:], EAS, [], 0.0)
-        V("ms", T.EA[:, E16(4)], ["EA4"], [], 1.0)
-        fcol(20, 1, 1.0, -32.0 / 4096, A.is_equal, A.mult)
-        for r, c in ((2, 2.0), (3, 32.0), (4, 480.0)):
-            fcol(21, 1, float(r), c / 4096, A.is_equal, A.mult)
-            tt(col(20), [("cF", 20, 21)], col(20), col(21), [("cF", 20, 22)], A.add)
-        fcol(22, 1, 0.0, None, A.is_equal)
-        ts(T.mB0[:], ["mB0"], T.cBM[:], ["cBM", ("cF", 22, 23)], col(22), None, A.mult)
-        const_r(0)
-        V("cp", T.mIF[:], ["mIF"], ["mI"], T.mI[:])
         ts(T.mCX[0:64, :], ["mCX0"], T.mCV[0:64, :], ["mCV"], 32.0, None, A.mult)
         V("ms", T.mCX[64:128, :], ["mCX1"], [], 15.0 / 128)
 
-    def constants3():
-        ts(T.cDUM[:], ["cDUM"], T.cG[:], ["cG", ("cF", 1, 2)], 16.0, col(1), A.mult, A.add)
-        ts(T.cDUM[:], ["cDUM"], T.cDUM[:], ["cDUM"], float(DUMMY), None, A.add)
-        fcol(23, 2, 0.0, None, A.is_equal)
+    def constants_b():
+        S(T.mEX[:], T.mE[:], ["mEX"], ["mE"], F.Copy, scale=16.0)
+        fcol(20, 1, 0.0, 1.0 / 4096, A.is_equal, A.mult)
+        for r, x in ((1, 16.0), (2, 256.0), (7, 8192.0)):
+            fcol(21 + r, 1, float(r), x / 4096, A.is_equal, A.mult)
+        for r in (1, 2, 7):
+            tt(col(20), [("cF", 20, 21)], col(20), col(21 + r), [("cF", 20, 29)], A.add)
+        S(T.mEL[:], T.mE[:], ["mEL"], ["mE", ("cF", 20, 21)], F.Copy, scale=col(20))
+
+    def constants_c():
         V("ms", T.EB[:], ["EB"], [], 1.0)
         ts(T.X1[:], ["X1"], T.cG[:], ["cG"], 1, None, SHR)
-        ts(T.KV[:, 0:1], ["KV"], T.cP[:], ["cP"], 31, None, AND)
-        V("cp", col(24), [("cF", 24, 25)], ["KV"], T.KV[:, 0:1])
-        ts(T.EB[:, E16(6)], ["EB"], T.X1[:], ["X1", ("cF", 24, 25)], 32.0, col(24), A.mult, A.add)
-        fcol(25, 1, 3.0, 512.0, A.is_lt, A.mult)
-        fcol(26, 1, 3.0, -256.0, A.is_ge, A.mult)
-        fcol(27, 1, 6.0, 255.0, A.is_ge, A.mult)
-        fcol(28, 1, 7.0, -16383.0, A.is_ge, A.mult)
-        fcol(29, 1, 8.0, 16384.0, A.is_ge, A.mult)
-        for k in (27, 28, 29):
-            tt(col(26), [("cF", 26, 27)], col(26), col(k), [("cF", 26, 30)], A.add)
-        fcol(30, 1, 8.0, -256.0, A.is_ge, A.mult)
-        fcol(31, 1, 11.0, 257.0, A.is_ge, A.mult)
-        fcol(32, 1, 12.0, -1.0, A.is_ge, A.mult)
-        for k in (31, 32):
-            tt(col(30), [("cF", 30, 31)], col(30), col(k), [("cF", 30, 33)], A.add)
-        ts(T.mXX[:], ["mXX"], T.cD[:], ["cD", ("cF", 25, 26)], 256.0, col(25), A.is_equal, A.mult)
-        ts(T.cA[:], ["cA"], T.cD[:], ["cD", ("cF", 26, 27)], 261.0, col(26), A.is_equal, A.mult)
-        tt(T.mXX[:], ["mXX"], T.mXX[:], T.cA[:], ["mXX", "cA"], A.add)
-        ts(T.cA[:], ["cA"], T.cD[:], ["cD", ("cF", 30, 31)], 251.0, col(30), A.is_equal, A.mult)
-        tt(T.mXX[:], ["mXX"], T.mXX[:], T.cA[:], ["mXX", "cA"], A.add)
-        ts(col(33), [("cF", 33, 34)], col(3), ["cF"], 16.0, col(4), A.mult, A.add)
+        fcol(30, 2, 0.0, None, A.is_equal)
+        ts(T.EB[:, E16(6)], ["EB"], T.X1[:], ["X1", ("cF", 7, 8)], 32.0, col(7), A.mult, A.add)
+        ts(T.cDUM[:], ["cDUM"], T.cG[:], ["cG", ("cF", 1, 2)], 16.0, col(1), A.mult, A.add)
+        fcol(33, 3, 16.0, col(4), A.mult, A.add)
+
+    def constants_d():
+        ts(T.cDUM[:], ["cDUM"], T.cDUM[:], ["cDUM"], float(DUMMY), None, A.add)
+        for a in range(1, 4):
+            fcol(33 + a, 33, 32.0 * a, None, A.add)
         for s in range(4):
             fcol(40 + s, 6, float(s), None, A.is_equal)
         for a in range(4):
-            if a:
-                fcol(33 + a, 33, 32.0 * a, None, A.add)
-            ts(T.mLM[:, 128 * a:128 * a + 128], ["mLM"], T.cM[:], ["cM", ("cF", 33 + a, 34 + a)], col(33 + a), 8192.0, A.is_equal, A.mult)
-        for s in range(2):
-            for gm in range(2):
-                k = 2 * s + gm
-                ts(T.mLX[:, 128 * k:128 * k + 128], ["mLX"], T.cD[:], ["cD", "cF"], 256.0 + 16 * (gm - s), col(23 if s == 0 else 2), A.is_equal, A.mult)
-
-    n64 = C // CH
+            ts(blk("mLM", a)[0], [blk("mLM", a)[1]], T.cM[:], ["cM", ("cF", 33 + a, 34 + a)], col(33 + a), 8192.0, A.is_equal, A.mult)
 
     def votes(k):
         lo, hi = 1024 * k, 1024 * k + 1024
         for i in range(16):
-            MM(T.bk3[:, n64 * k:n64 * (k + 1)], T.mE[:, 128 * i:128 * i + 128], T.R[:, lo + i:hi:16], False, False, "bk3", [("mE", 128 * i, 128 * i + 128), ("R", lo, hi)])
+            MM(T.bk3[:, NT * k:NT * (k + 1)], blk("mE", i)[0], T.R[:, lo + i:hi:16], False, False, "bk3", [blk("mE", i)[1], ("R", lo, hi)])
 
     for t in range(RO):
-        first = t == 0
+        first, more = t == 0, t < RO - 1
         TB = "TB%d" % t
         MM(T.bk2[:, 0:C], T.mCH[:], T.mON[:], True, False, "bk2", ["mCH", "mON"])
         MM(T.bk2[:, 0:C], T.mP256[:], T.P[:], False, False, "bk2", ["mP256", "P"])
         for k in range(CH):
             lo, hi = 1024 * k, 1024 * k + 1024
-            off = T.OFF[:, n64 * k:n64 * (k + 1)]
-            tt(T.M[:, lo:hi], [("M", lo, hi)], T.U[:].indirect(off), T.PXP[:, lo:hi], ["U", ("OFF", n64 * k, n64 * (k + 1))] + allpx, A.max)
-            S(T.R[:, lo:hi], T.U[:].indirect(off), [("R", lo, hi)], ["U", ("OFF", n64 * k, n64 * (k + 1))], F.Copy)
-            if first and k == 0:
-                constants()
-            if first and k == 1:
-                codes2(0)
-            if k == 0 and not first:
-                pass
+            off, offr = T.OFF[:, NT * k:NT * (k + 1)], ("OFF", NT * k, NT * (k + 1))
+            tt(T.M[:, lo:hi], [("M", lo, hi)], T.U[:].indirect(off), T.PXP[:, lo:hi], ["U", offr] + allpx, A.max)
+            S(T.R[:, lo:hi], T.U[:].indirect(off), [("R", lo, hi)], ["U", offr], F.Copy)
             for i in range(16):
-                MM(T.bk2[:, n64 * k:n64 * (k + 1)], T.mI16[:], T.M[:, lo + i:hi:16], False, k == CH - 1 and i == 15, "bk2", ["mI16", ("M", lo, hi)])
+                MM(T.bk2[:, NT * k:NT * (k + 1)], T.mI16[:], T.M[:, lo + i:hi:16], False, k == CH - 1 and i == 15, "bk2", ["mI16", ("M", lo, hi)])
             if k == 0:
                 MM(T.bk3[:, 0:C], T.mCV[:], T.mON[:], True, False, "bk3", ["mCV", "mON"])
             else:
                 votes(k - 1)
+        if first:
+            codes2(0)
         votes(CH - 1)
         MM(T.bk3[:, 0:C], T.mI[:], T.N4[:], False, True, "bk3", ["mI", "N4"])
         if first:
-            constants2()
+            constants_a()
 
         V("tr", T.KT[:], ["KT"], ["bk2"], T.bk2[:, 0:C])
         V("sc", T.S1[:], ["S1"], ["cMASK", "KT"], T.cMASK[:], T.KT[:], 0.0, A.mult, A.max)
+        for gm in range(2):
+            ts(T.LB[:, gm:16:2], ["LB%d" % gm], T.S1[:, 15 + 16 * gm:C:32], ["S1", "LIM"], T.LIM[:, gm:gm + 1], BIG, A.is_lt, A.mult)
+        LBS = ["LB0", "LB1"]
+        tt(T.TAU[:], ["TAU"], T.LB[:], T.S1[:, 15:C:16], LBS + ["S1"], A.max)
+        S(T.TV[:], T.LB[:], ["TV"], LBS + [("cF", 59, 64)], scale=-1.0, bias=col(59))
         l3 = T.EA[:, E16(3)]
-        tt(l3, ["EA3"], T.S1[:, 15:C:16], T.LIM[:], ["S1", "LIM"], A.is_lt)
-        ts(T.LB[:], ["LB"], l3, ["EA3"], BIG, None, A.mult)
-        tt(T.TAU[:], ["TAU"], T.LB[:], T.S1[:, 15:C:16], ["LB", "S1"], A.max)
+        S(l3, T.LB[:], ["EA3"], LBS, F.Sign)
         tt(T.WT[:], ["WT"], T.TAU[:].indirect(T.cBL[:]), T.KT[:], ["TAU", "cBL", "KT"], A.is_le)
         V("tr", T.bk4[:, 0:C], ["bk4"], ["WT"], T.WT[:])
-        ts(T.X1[:], ["X1"], T.TAU[:], ["TAU"], 15, None, AND)
-        ts(T.X2[:], ["X2"], T.TAU[:], ["TAU"], 4, 15, SHR, AND)
-        V("cp", T.EA[:, E16(1)], ["EA1"], ["X1"], T.X1[:])
-        V("cp", T.EA[:, E16(2)], ["EA2"], ["X2"], T.X2[:])
-        V("tr", T.VT[:], ["VT"], ["bk3"], T.bk3[:, 0:C])
-        V("sc", T.S2[:], ["S2"], ["cNEG", "VT"], T.cNEG[:], T.VT[:], 0.0, A.add, A.max)
-        V("cp", T.KV[:], ["KV"], ["S2"], T.S2[:, 15:C:16])
-        ts(T.ZV[:], ["ZV"], T.S2[:, 15:C:16], ["S2"], 0.0, None, A.is_ge)
-        ts(T.NB[:], ["NB"], T.KV[:], ["KV"], 255, None, AND)
-        tt(T.ZV[:], ["ZV"], T.ZV[:], l3, ["ZV", "EA3"], A.mult)
-        ts(T.TK[:], ["TK"], T.NB[:], ["NB"], 2.0, -512.0, A.mult, A.add)
-        tt(T.EA[:, E16(0)], ["EA0"], T.TK[:], T.ZV[:], ["TK", "ZV"], A.mult)
-        V("tr", T.EN[:], ["EN"], EAS, T.EA[:])
-        MM(T.bk0[:, 0:C], T.mB0[:], T.EN[:], True, True, "bk0", ["mB0", "EN"])
-        MM(T.bk1[:, 0:C], T.mNR[:, 128 * t:128 * t + 128], T[TB][:], True, False, "bk1", [("mNR", 128 * t, 128 * t + 128), TB])
-        MM(T.bk1[:, 0:C], T.mBR[:, 128 * t:128 * t + 128], T.EN[:], False, True, "bk1", [("mBR", 128 * t, 128 * t + 128), "EN"])
-
-        if t < RO - 1:
+        if more:
             MM(T.bk6[:, 0:16], T.mON[:, 0:128], l3, True, True, "bk6", ["mON", "EA3"])
             S(T.MJK[:], T.bk6[:, 0:16], ["MJK", "MC"], ["bk6"], scale=16.0, accum_out=T.MC[:])
-            S(T.MA[:], T.MC[:], ["MA"], ["MC", ("cF", 60, 64)], scale=1.0 / 16, bias=col(63))
-            S(T.MQ[:], T.MA[:], ["MQ"], ["MA", ("cF", 60, 64)], scale=1.0 / 256, bias=col(61))
-            S(T.MR[:], T.MQ[:], ["MR"], ["MQ", ("cF", 60, 64)], bias=col(62))
+            S(T.MA[:], T.MC[:], ["MA"], ["MC", ("cF", 59, 64)], scale=1.0 / 16, bias=col(63))
+            S(T.MQ[:], T.MA[:], ["MQ"], ["MA", ("cF", 59, 64)], scale=1.0 / 256, bias=col(61))
+            S(T.MR[:], T.MQ[:], ["MR"], ["MQ", ("cF", 59, 64)], bias=col(62))
             S(T.MF[:], T.MR[:], ["MF"], ["MR", "MC"], scale=-4096.0, bias=T.MC[:])
+        if first:
+            constants_b()
 
         MM(T.bk5[:, 0:C], T.mIF[:], T.CM[:], True, False, "bk5", ["mIF", "CM"])
         MM(T.bk5[:, 0:C], T.mCX[:], T.mON[:], False, False, "bk5", ["mCX0", "mCX1", "mON"])
-
-        def pick(i):
-            tt(T.PR[:, i:W:16], ["PR%d" % i], T.R[:, i:W:16], T.bk4[:, 0:C], ["R", "bk4"], A.mult)
-            MM(T.bk5[:, 0:C], T.mEX[:, 128 * i:128 * i + 128], T.PR[:, i:W:16], False, i == 15, "bk5", ["mEX", "PR%d" % i])
-        for i in range(4):
-            pick(i)
         a, b = C * t, C * t + C
-        tt(T.DL[:], ["DL"], T.FN[:], T.bk0[:, 0:C], ["FN", "bk0"], A.mult)
-        tt(T.TS[:, a:b], [("TS", a, b)], T.DL[:], T.bk1[:, 0:C], ["DL", "bk1"], A.add)
-        dst = T.cores[(rank + 1) % N] if t < RO - 1 else T.cores[(rank - (RO - 1)) % N]
-        rid, pid, _se = topo.addr(dst)
-        mask = topo.mask(core, dst)
-        src = T.cores[(rank - 1) % N] if t < RO - 1 else T.cores[(rank + RO - 1) % N]
-        order("g", [("TS", a, b)], [], "snd", 0)
-        g.remote_dma(T["TB%d" % (t + 1)][:], T.TS[:, a:b], T.sem["arr%d" % (t + 1)], T.sem["snd"], pid, rid, mask)
-        arrive("TB%d" % (t + 1), "arr%d" % (t + 1), len(topo.engines(src, core)))
-        for i in range(4, 16):
-            pick(i)
+
+        def spread():
+            V("tr", T.EN[:], ["EN"], EAS, T.EA[:])
+            MM(T.bk0[:, 0:C], T.mB0[:], T.EN[:], True, True, "bk0", ["mB0", "EN"])
+            MM(T.bk1[:, 0:C], blk("mNR", t)[0], T[TB][:], True, False, "bk1", [blk("mNR", t)[1], TB])
+            MM(T.bk1[:, 0:C], blk("mBR", t)[0], T.EN[:], False, True, "bk1", [blk("mBR", t)[1], "EN"])
+
+        def leave():
+            tt(T.TS[:, a:b], [("TS", a, b)], T.DL[:], T.bk1[:, 0:C], ["DL", "bk1"], A.add)
+            step = 1 if more else -(RO - 1)
+            dst, src = T.cores[(rank + step) % N], T.cores[(rank - step) % N]
+            rid, pid, _se = topo.addr(dst)
+            order("g", [("TS", a, b)], [])
+            g.remote_dma(T["TB%d" % (t + 1)][:], T.TS[:, a:b], T.sem["arr%d" % (t + 1)], T.sem["snd"], pid, rid, topo.mask(core, dst))
+            last["TB%d" % (t + 1)] = [(0, 1 << 20, True, "r", "arr%d" % (t + 1), len(topo.engines(src, core)))]
+            for u in range(1 if first else t + 2, min(t + 3, RO)):
+                icodes(u)
+        chain = [
+            lambda: ts(T.X1[:], ["X1"], T.TAU[:], ["TAU"], 15, None, AND),
+            lambda: ts(T.X2[:], ["X2"], T.TAU[:], ["TAU"], 4, 15, SHR, AND),
+            lambda: V("tr", T.VT[:], ["VT"], ["bk3"], T.bk3[:, 0:C]),
+            lambda: V("cp", T.EA[:, E16(1)], ["EA1"], ["X1"], T.X1[:]),
+            lambda: V("sc", T.S2[:], ["S2"], ["cNEG", "VT"], T.cNEG[:], T.VT[:], 0.0, A.add, A.max),
+            lambda: V("cp", T.EA[:, E16(2)], ["EA2"], ["X2"], T.X2[:]),
+            lambda: V("cp", T.KV[:], ["KV"], ["S2"], T.S2[:, 15:C:16]),
+            lambda: tt(T.EA[:, E16(5)], ["EA5"], T.S2[:, 15:C:16], T.TV[:], ["S2", "TV"], A.is_ge),
+            lambda: ts(T.NB[:], ["NB"], T.KV[:], ["KV"], 255, None, AND),
+            lambda: tt(T.EA[:, E16(0)], ["EA0"], T.NB[:], T.EA[:, E16(5)], ["NB", "EA5"], A.mult),
+            spread,
+            None,
+            lambda: tt(T.DL[:], ["DL"], T.FN[:], T.bk0[:, 0:C], ["FN", "bk0"], A.mult),
+            leave,
+        ]
+        for i in range(16):
+            tt(T.PR[:, i:W:16], ["PR%d" % i], T.R[:, i:W:16], T.bk4[:, 0:C], ["R", "bk4"], A.mult)
+            MM(T.bk5[:, 0:C], blk("mEX", i)[0], T.PR[:, i:W:16], False, i == 15, "bk5", ["mEX", "PR%d" % i])
+            if i < len(chain) and chain[i] is not None:
+                chain[i]()
         S(T.W1[:], T.bk4[:, 0:C], ["W1"], ["bk4"], scale=-1.0, bias=1.0)
-        if first:
-            constants3()
-        if t < RO - 1:
+        if more:
             ts(T.LIM[:], ["LIM"], T.TH16[:], ["TH16", "MF"], T.MF[:], None, A.add)
+        if first:
+            constants_c()
 
         V("tr", T.XT[:], ["XT"], ["bk5"], T.bk5[:, 0:C])
         V("sc", T.S3[:], ["S3"], ["cNEG", "XT"], T.cNEG[:], T.XT[:], 0.0, A.add, A.max)
+        if more:
+            if first:
+                const_t(1)
+                const_g(1)
+            codes(t + 1)
         V("cp", T.KI[:], ["KI"], ["S3"], T.S3[:, 15:C:16])
-        ts(T.ZK[:], ["ZK"], T.S3[:, 15:C:16], ["S3"], 0.0, None, A.is_lt)
+        tt(T.EB[:, E16(7)], ["EBz"], T.S3[:, 15:C:16], T.LB[:], ["EB", "S3"] + LBS, A.is_lt)
         for r in range(3):
             ts(T["D%d" % r][:], ["D%d" % r], T.KI[:], ["KI"], 4 * r, 15, SHR, AND)
-        tt(T.ZZ[:], ["ZZ"], T.ZK[:], l3, ["ZK", "EA3"], A.max)
         for r in range(3):
             V("cp", T.EB[:, E16(r)], ["EBd%d" % r], ["EB", "D%d" % r], T["D%d" % r][:])
             S(T.EB[:, E16(3 + r)], T.EB[:, E16(r)], ["EBs%d" % r], ["EB", "EBd%d" % r], F.Square)
-        V("cp", T.EB[:, E16(7)], ["EBz"], ["EB", "ZZ"], T.ZZ[:])
-        ts(T.XC[:], ["XC"], T.KI[:], ["KI"], 4095, None, AND)
-        ts(T.ZK[:], ["ZK"], T.ZZ[:], ["ZZ"], 8192.0, None, A.mult)
-        tt(T.XF[:], ["XF"], T.XC[:], T.ZK[:], ["XC", "ZK"], A.add)
+        if more:
+            codev(t + 1, 0)
         V("tr", T.VN[:], ["VN"], ["EB", "EBz"] + ["EBd%d" % r for r in range(3)] + ["EBs%d" % r for r in range(3)], T.EB[:])
         MM(T.bk7[:, 0:C], T.mXX[:], T.VN[:], True, True, "bk7", ["mXX", "VN"])
-        ts(T.VM[:, 0:2 * C:2], ["VM0"], T.VN[:], ["VN", ("cF", 23, 24)], col(23), None, A.mult)
+        ts(T.VM[:, 0:2 * C:2], ["VM0"], T.VN[:], ["VN", ("cF", 30, 31)], col(30), None, A.mult)
         ts(T.VM[:, 1:2 * C:2], ["VM1"], T.VN[:], ["VN", ("cF", 2, 3)], col(2), None, A.mult)
         S(T.RV[:], T.bk7[:, 0:C], ["RV"], ["bk7"], F.Copy)
-        if t < RO - 1:
-            if first:
-                const_t(1)
-            codes(t + 1)
-            const_r(t + 1)
-            if t + 2 < RO:
-                const_t(t + 2)
+        for k in range(16):
+            MM(T.bk6[:, 0:16], blk("mEL", k)[0], T.VN[:, k:C:16], k == 0, False, "bk6", ["mEL", "VN"])
+        if more:
+            codev(t + 1, 1)
+        if first:
+            constants_d()
+        if t + 2 < RO:
+            const_t(t + 2)
+            const_g(t + 2)
         banks = ["bk2", "bk3", "bk4", "bk5", "bk7"]
         use = [0]
-
-        def block(a, be):
-            bank = banks[use[0] % len(banks)]
-            use[0] += 1
-            n = 64 * (be + 1)
-            MM(T[bank][:, 0:n], T.VM[32 * a:32 * a + 32, 128 * be:128 * be + 128], T.RV[32 * a:32 * a + 32, 0:n], True, True, bank, ["VM0", "VM1", "RV"])
-            k = 4 * a + be
-            if (a, be) in S_RED:
-                S(T.JK[:, 0:n], T[bank][:, 0:n], ["JK", ("FL", k, k + 1)], [bank], F.Relu, accum_out=T.FL[:, k:k + 1])
-            else:
-                V("rd", T.FL[:, k:k + 1], [("FL", k, k + 1)], [bank], T[bank][:, 0:n], AxisListType.X, A.max)
         for be in (3, 2, 1, 0):
-            for a in range(4):
-                block(a, be)
-        for s in range(2):
-            for gm in range(2):
-                k = 2 * s + gm
-                MM(T.bk6[:, s:16:2], T.mLX[:, 128 * k:128 * k + 128], T.XF[:, gm:16:2], gm == 0, gm == 1, "bk6", ["mLX", "XF"])
-        tt(T.XL[:], ["XL"], T.cDUM[:], T.bk6[:, 0:16], ["cDUM", "bk6"], A.min)
+            for a4 in range(4):
+                bank = banks[use[0] % len(banks)]
+                use[0] += 1
+                n, k = 64 * (be + 1), 4 * a4 + be
+                rows = slice(32 * a4, 32 * a4 + 32)
+                MM(T[bank][:, 0:n], T.VM[rows, 128 * be:128 * be + 128], T.RV[rows, 0:n], True, True, bank, ["VM0", "VM1", "RV"])
+                if (a4, be) in S_RED:
+                    S(T.JK[:, 0:n], T[bank][:, 0:n], ["JK", ("FL", k, k + 1)], [bank], F.Relu, accum_out=T.FL[:, k:k + 1])
+                else:
+                    V("rd", T.FL[:, k:k + 1], [("FL", k, k + 1)], [bank], T[bank][:, 0:n], AxisListType.X, A.max)
+        if more:
+            codev(t + 1, 2)
         for s in range(4):
-            ts(T.FB[:, s:64:4], ["FB%d" % s], T.FL[:], ["FL", ("cF", 40 + s, 41 + s)], 0.0, col(40 + s), A.is_gt, A.mult)
-        for a in range(4):
-            MM(T.bk7[:, 0:16], T.mLM[:, 128 * a:128 * a + 128], T.FB[:, 16 * a:16 * a + 16], a == 0, a == 3, "bk7", ["mLM"] + ["FB%d" % s for s in range(4)])
-        if t < RO - 1:
-            codesv(t + 1)
-        tt(T.YL[:], ["YL"], T.XL[:], T.bk7[:, 0:16], ["XL", "bk7"], A.add)
-        tt(T.YM[:], ["YM"], T.YL[:], T.cDUM[:], ["YL", "cDUM"], A.min)
+            if s < 2:
+                S(T.FB[:, s:64:4], T.FL[:], ["FB%d" % s], ["FL", ("cF", 40 + s, 41 + s)], F.Relu, scale=col(40 + s))
+            else:
+                ts(T.FB[:, s:64:4], ["FB%d" % s], T.FL[:], ["FL", ("cF", 40 + s, 41 + s)], 0.0, col(40 + s), A.is_gt, A.mult)
+        for a4 in range(4):
+            MM(T.bk6[:, 0:16], blk("mLM", a4)[0], T.FB[:, 16 * a4:16 * a4 + 16], False, a4 == 3, "bk6", ["mLM"] + ["FB%d" % s for s in range(4)])
+        if more:
+            codev(t + 1, 3)
+        tt(T.YM[:], ["YM"], T.cDUM[:], T.bk6[:, 0:16], ["cDUM", "bk6"], A.min)
         V("cp", T.OL[:], ["OL"], ["YM"], T.YM[:])
         S(T.UG[:], T.U[:].indirect(T.OL[:]), ["UG"], ["U", "OL"], F.Copy)
-        if t < RO - 1:
-            codesw(t + 1)
+        if more:
+            codev(t + 1, 4)
             codes2(t + 1)
         tt(T.U[:].indirect(T.OL[:]), ["U"], T.UG[:], T.W1[:], ["UG", "W1", "OL"], A.mult)
 
@@ -500,4 +493,4 @@ def rank_program(g, core, T, topo):
     dma("y", 5, T.yc[:], T.OUTC[:], ["OUTC"], ["yc"])
     need("y", "dma4", 16)
     need("y", "dma5", 16)
-    g.wait_ge(T.sem["snd"], sum(len(topo.engines(core, T.cores[(rank + 1) % N] if t < RO - 1 else T.cores[(rank - (RO - 1)) % N])) for t in range(RO)))
+    g.wait_ge(T.sem["snd"], sum(len(topo.engines(core, T.cores[(rank + (1 if t < RO - 1 else 1 - RO)) % N])) for t in range(RO)))

@@ -12,7 +12,6 @@ BIG = 2.0 ** 25
 MAGIC = 1.5 * 2.0 ** 23
 CH = 4
 NT = C // CH
-S_RED = [(a, b) for a in range(4) for b in range(4) if b != 1 and (a, b) not in ((3, 3), (3, 0))]
 RHO = [(5 * t) % 16 for t in range(RO)]
 
 SCRATCH = {}
@@ -264,23 +263,25 @@ def rank_program(g, core, T, topo):
     S(T.mP256[:], T.mI[:], ["mP256"], ["mI"], F.Copy, scale=-256.0)
     ts(T.cJ[:], ["cJ"], T.cM[:], ["cM"], 15, None, AND)
     ts(T.mCH[:], ["mCH"], T.cJ[:], ["cJ"], -1.0 / 128, 15.0 / 128, A.mult, A.add)
-    ts(T.cB[:], ["cB"], T.cJ[:], ["cJ"], 1.0, None, A.mult)
     ts(T.mCV[:], ["mCV"], T.cJ[:], ["cJ"], -2.0, 30.0, A.mult, A.add)
-    tt(T.cMI[:], ["cMI"], T.cB[:], T.cA[:], ["cB", "cA"], A.add)
-    ts(T.cB[:], ["cB"], T.cD[:], ["cD"], 256.0, -1.0, A.is_gt, A.mult)
-    V("ms", T.mZ[:], ["mZ"], [], 0.0)
-    tt(T.cB[:], ["cB"], T.cB[:], T.cBM[:], ["cB", "cBM"], A.mult)
-    V("ms", T.mXX[:], ["mXX"], [], 0.0)
-    tt(T.mF0[:], ["mF0"], T.cB[:], T.mI[:], ["cB", "mI"], A.add)
-    for i in range(16):
-        ts(blk("mE", i)[0], [blk("mE", i)[1]], T.cMI[:], ["cMI"], float(i), 4096.0, A.is_equal, A.mult)
-    const_g(0)
-    fill("mB0", 0, [[-16, 8], [0, 16]], 0, 1, 2.0, "mZ", 0)
-    fill("mB0", 0, [[-16, 8], [0, 16]], -5, 1, -512.0)
-    for r, m, x in [(k, k, 512.0) for k in range(3)] + [(3 + k, 8 + k, -256.0) for k in range(3)] + [(8 + k, 3 + k, -256.0) for k in range(3)] + \
-            [(6, 11, -1.0), (11, 6, 1.0), (7, 12, -16384.0)]:
-        cell("mXX", 0, r, m, x)
     S(T.mIF[:], T.mI[:], ["mIF"], ["mI"], F.Copy)
+
+    def constants_0():
+        ts(T.cB[:], ["cB"], T.cJ[:], ["cJ"], 1.0, None, A.mult)
+        ts(T.cT[:], ["cT"], T.cD[:], ["cD"], 256.0, None, A.is_gt)
+        V("ms", T.mZ[:], ["mZ"], [], 0.0)
+        tt(T.cMI[:], ["cMI"], T.cB[:], T.cA[:], ["cB", "cA"], A.add)
+        tt(T.cB[:], ["cB"], T.cT[:], T.cBM[:], ["cT", "cBM"], A.mult)
+        V("ms", T.mXX[:], ["mXX"], [], 0.0)
+        for i in range(16):
+            ts(blk("mE", i)[0], [blk("mE", i)[1]], T.cMI[:], ["cMI"], float(i), 4096.0, A.is_equal, A.mult)
+        tt(T.mF0[:], ["mF0"], T.mI[:], T.cB[:], ["cB", "mI"], A.subtract)
+        const_g(0)
+        fill("mB0", 0, [[-16, 8], [0, 16]], 0, 1, 2.0, "mZ", 0)
+        fill("mB0", 0, [[-16, 8], [0, 16]], -5, 1, -512.0)
+        for r, m, x in [(k, k, 512.0) for k in range(3)] + [(3 + k, 8 + k, -256.0) for k in range(3)] + [(8 + k, 3 + k, -256.0) for k in range(3)] + \
+                [(6, 11, -1.0), (11, 6, 1.0), (7, 12, -16384.0)]:
+            cell("mXX", 0, r, m, x)
 
     def constants_a():
         V("ms", T.cMASK[:], ["cMASK"], [], 1.0)
@@ -330,42 +331,106 @@ def rank_program(g, core, T, topo):
     def votes(k):
         lo, hi = 1024 * k, 1024 * k + 1024
         for i in range(16):
-            MM(T.bk3[:, NT * k:NT * (k + 1)], blk("mE", i)[0], T.R[:, lo + i:hi:16], False, False, "bk3", [blk("mE", i)[1], ("R", lo, hi)])
+            MM(T.bk2[:, NT * k:NT * (k + 1)], blk("mE", i)[0], T.R[:, lo + i:hi:16], False, False, "bk2", [blk("mE", i)[1], ("R", lo, hi)])
 
     for t in range(RO):
         first, more = t == 0, t < RO - 1
         TB = "TB%d" % t
-        MM(T.bk2[:, 0:C], T.mCH[:], T.mON[:], True, False, "bk2", ["mCH", "mON"])
-        MM(T.bk2[:, 0:C], T.mP256[:], T.P[:], False, False, "bk2", ["mP256", "P"])
-        for k in range(CH):
+        LBS = ["LB00", "LB10", "LB01", "LB11"]
+        l3 = T.EA[:, E16(3)]
+
+        def gather_v(c0, n):
+            lo, hi = 16 * c0, 16 * (c0 + n)
+            tt(T.M[:, lo:hi], [("M", lo, hi)], T.U[:].indirect(T.OFF[:, c0:c0 + n]), T.PXP[:, lo:hi], ["U", ("OFF", c0, c0 + n)] + allpx, A.max)
+
+        def gather_s(k):
             lo, hi = 1024 * k, 1024 * k + 1024
-            off, offr = T.OFF[:, NT * k:NT * (k + 1)], ("OFF", NT * k, NT * (k + 1))
-            tt(T.M[:, lo:hi], [("M", lo, hi)], T.U[:].indirect(off), T.PXP[:, lo:hi], ["U", offr] + allpx, A.max)
-            S(T.R[:, lo:hi], T.U[:].indirect(off), [("R", lo, hi)], ["U", offr], F.Copy)
+            S(T.R[:, lo:hi], T.U[:].indirect(T.OFF[:, NT * k:NT * k + NT]), [("R", lo, hi)], ["U", ("OFF", NT * k, NT * k + NT)], F.Copy)
+
+        def gains(k):
+            lo, hi, bank, c0 = 1024 * k, 1024 * k + 1024, ("bk0", "bk1")[k // 2], NT * (k % 2)
             for i in range(16):
-                MM(T.bk2[:, NT * k:NT * (k + 1)], T.mI16[:], T.M[:, lo + i:hi:16], False, k == CH - 1 and i == 15, "bk2", ["mI16", ("M", lo, hi)])
-            if k == 0:
-                MM(T.bk3[:, 0:C], T.mCV[:], T.mON[:], True, False, "bk3", ["mCV", "mON"])
+                MM(T[bank][:, c0:c0 + NT], T.mI16[:], T.M[:, lo + i:hi:16], False, k % 2 == 1 and i == 15, bank, ["mI16", ("M", lo, hi)])
+
+        def level(h, step):
+            a, b, a8 = 128 * h, 128 * h + 128, 8 * h
+            kt, s1, tau, wt = ("KT", a, b), ("S1", a, b), ("TAU", a8, a8 + 8), ("WT", a, b)
+            gb, wb = ("bk0", "bk1")[h], ("bk3", "bk4")[h]
+            if step == 0:
+                V("tr", T.KT[:, a:b], [kt], [gb], T[gb][:, 0:128])
+            elif step == 1:
+                V("sc", T.S1[:, a:b], [s1], ["cMASK", kt], T.cMASK[:, 0:128], T.KT[:, a:b], 0.0, A.mult, A.max)
+            elif step == 2:
+                for gm in range(2):
+                    ts(T.LB[:, a8 + gm:a8 + 8:2], ["LB%d%d" % (gm, h)], T.S1[:, a + 15 + 16 * gm:b:32], [s1, "LIM"], T.LIM[:, gm:gm + 1], BIG, A.is_lt, A.mult)
+            elif step == 3:
+                tt(T.TAU[:, a8:a8 + 8], [tau], T.LB[:, a8:a8 + 8], T.S1[:, a + 15:b:16], ["LB0%d" % h, "LB1%d" % h, s1], A.max)
+            elif step == 4:
+                tt(T.WT[:, a:b], [wt], T.TAU[:, a8:a8 + 8].indirect(T.cBL[:, 0:8]), T.KT[:, a:b], [tau, "cBL", kt], A.is_le)
             else:
-                votes(k - 1)
-        if first:
-            codes2(0)
-        votes(CH - 1)
-        MM(T.bk3[:, 0:C], T.mI[:], T.N4[:], False, True, "bk3", ["mI", "N4"])
+                V("tr", T[wb][:, 0:128], [wb], [wt], T.WT[:, a:b])
+
+        for h in range(2):
+            gb = ("bk0", "bk1")[h]
+            MM(T[gb][:, 0:128], T.mCH[:], T.mON[:, 0:128], True, False, gb, ["mCH", "mON"])
+            MM(T[gb][:, 0:128], T.mP256[:], T.P[:, 128 * h:128 * h + 128], False, False, gb, ["mP256", "P"])
+        MM(T.bk2[:, 0:C], T.mCV[:], T.mON[:], True, False, "bk2", ["mCV", "mON"])
+        for k in range(2):
+            gather_v(NT * k, NT)
+            gather_s(k)
+            if first and k == 0:
+                constants_0()
+            gains(k)
+        votes(0)
         if first:
             constants_a()
+        gather_v(128, 32)
+        gather_s(2)
+        level(0, 0)
+        gather_v(160, 32)
+        gains(2)
+        votes(1)
+        level(0, 1)
+        gather_s(3)
+        for k in range(4):
+            gather_v(192 + 16 * k, 16)
+            level(0, 2 + k)
+        gains(3)
+        votes(2)
+        if first:
+            codes2(0)
+        votes(3)
+        MM(T.bk2[:, 0:C], T.mI[:], T.N4[:], False, True, "bk2", ["mI", "N4"])
+        if first:
+            constants_b()
 
-        V("tr", T.KT[:], ["KT"], ["bk2"], T.bk2[:, 0:C])
-        V("sc", T.S1[:], ["S1"], ["cMASK", "KT"], T.cMASK[:], T.KT[:], 0.0, A.mult, A.max)
-        for gm in range(2):
-            ts(T.LB[:, gm:16:2], ["LB%d" % gm], T.S1[:, 15 + 16 * gm:C:32], ["S1", "LIM"], T.LIM[:, gm:gm + 1], BIG, A.is_lt, A.mult)
-        LBS = ["LB0", "LB1"]
-        tt(T.TAU[:], ["TAU"], T.LB[:], T.S1[:, 15:C:16], LBS + ["S1"], A.max)
-        S(T.TV[:], T.LB[:], ["TV"], LBS + [("cF", 59, 64)], scale=-1.0, bias=col(59))
-        l3 = T.EA[:, E16(3)]
-        S(l3, T.LB[:], ["EA3"], LBS, F.Sign)
-        tt(T.WT[:], ["WT"], T.TAU[:].indirect(T.cBL[:]), T.KT[:], ["TAU", "cBL", "KT"], A.is_le)
-        V("tr", T.bk4[:, 0:C], ["bk4"], ["WT"], T.WT[:])
+        def pick(h, i):
+            pr, xb, wb = "PR%d_%d" % (h, i), ("bk5", "bk7")[h], ("bk3", "bk4")[h]
+            lo, hi = 2048 * h, 2048 * h + 2048
+            tt(T.PR[:, lo + i:hi:16], [pr], T.R[:, lo + i:hi:16], T[wb][:, 0:128], [("R", lo, hi), wb], A.mult)
+            MM(T[xb][:, 0:128], blk("mEX", i)[0], T.PR[:, lo + i:hi:16], False, i == 15, xb, ["mEX", pr])
+
+        for h in range(2):
+            xb = ("bk5", "bk7")[h]
+            MM(T[xb][:, 0:128], T.mIF[:], T.CM[:, 128 * h:128 * h + 128], True, False, xb, ["mIF", "CM"])
+            MM(T[xb][:, 0:128], T.mCX[:], T.mON[:, 0:128], False, False, xb, ["mCX0", "mCX1", "mON"])
+        vote = {
+            9: lambda: ts(T.X1[:], ["X1"], T.TAU[:], ["TAU"], 15, None, AND),
+            10: lambda: V("tr", T.VT[:], ["VT"], ["bk2"], T.bk2[:, 0:C]),
+            12: lambda: V("sc", T.S2[:], ["S2"], ["cNEG", "VT"], T.cNEG[:], T.VT[:], 0.0, A.add, A.max),
+            13: lambda: ts(T.X2[:], ["X2"], T.TAU[:], ["TAU"], 4, 15, SHR, AND),
+            14: lambda: V("cp", T.KV[:], ["KV"], ["S2"], T.S2[:, 15:C:16]),
+            15: lambda: ts(T.NB[:], ["NB"], T.KV[:], ["KV"], 255, None, AND),
+        }
+        for i in range(16):
+            pick(0, i)
+            if i % 2 == 1 and i < 12:
+                level(1, i // 2)
+                if i // 2 == 2:
+                    S(T.TV[:], T.LB[:], ["TV"], LBS + [("cF", 59, 64)], scale=-1.0, bias=col(59))
+                    S(l3, T.LB[:], ["EA3"], LBS, F.Sign)
+            if i in vote:
+                vote[i]()
         if more:
             MM(T.bk6[:, 0:16], T.mON[:, 0:128], l3, True, True, "bk6", ["mON", "EA3"])
             S(T.MJK[:], T.bk6[:, 0:16], ["MJK", "MC"], ["bk6"], scale=16.0, accum_out=T.MC[:])
@@ -373,11 +438,13 @@ def rank_program(g, core, T, topo):
             S(T.MQ[:], T.MA[:], ["MQ"], ["MA", ("cF", 59, 64)], scale=1.0 / 256, bias=col(61))
             S(T.MR[:], T.MQ[:], ["MR"], ["MQ", ("cF", 59, 64)], bias=col(62))
             S(T.MF[:], T.MR[:], ["MF"], ["MR", "MC"], scale=-4096.0, bias=T.MC[:])
-        if first:
-            constants_b()
 
-        MM(T.bk5[:, 0:C], T.mIF[:], T.CM[:], True, False, "bk5", ["mIF", "CM"])
-        MM(T.bk5[:, 0:C], T.mCX[:], T.mON[:], False, False, "bk5", ["mCX0", "mCX1", "mON"])
+        def claim(h, step):
+            x, s3, xb = ("XT", 128 * h, 128 * h + 128), ("S3", 128 * h, 128 * h + 128), ("bk5", "bk7")[h]
+            if step == 0:
+                V("tr", T.XT[:, x[1]:x[2]], [x], [xb], T[xb][:, 0:128])
+            else:
+                V("sc", T.S3[:, x[1]:x[2]], [s3], ["cNEG", x], T.cNEG[:, 0:128], T.XT[:, x[1]:x[2]], 0.0, A.add, A.max)
         a, b = C * t, C * t + C
 
         def spread():
@@ -397,34 +464,31 @@ def rank_program(g, core, T, topo):
             for u in range(1 if first else t + 2, min(t + 3, RO)):
                 icodes(u)
         chain = [
-            lambda: ts(T.X1[:], ["X1"], T.TAU[:], ["TAU"], 15, None, AND),
-            lambda: ts(T.X2[:], ["X2"], T.TAU[:], ["TAU"], 4, 15, SHR, AND),
-            lambda: V("tr", T.VT[:], ["VT"], ["bk3"], T.bk3[:, 0:C]),
-            lambda: V("cp", T.EA[:, E16(1)], ["EA1"], ["X1"], T.X1[:]),
-            lambda: V("sc", T.S2[:], ["S2"], ["cNEG", "VT"], T.cNEG[:], T.VT[:], 0.0, A.add, A.max),
-            lambda: V("cp", T.EA[:, E16(2)], ["EA2"], ["X2"], T.X2[:]),
-            lambda: V("cp", T.KV[:], ["KV"], ["S2"], T.S2[:, 15:C:16]),
             lambda: tt(T.EA[:, E16(5)], ["EA5"], T.S2[:, 15:C:16], T.TV[:], ["S2", "TV"], A.is_ge),
-            lambda: ts(T.NB[:], ["NB"], T.KV[:], ["KV"], 255, None, AND),
+            lambda: V("cp", T.EA[:, E16(1)], ["EA1"], ["X1"], T.X1[:]),
+            lambda: V("cp", T.EA[:, E16(2)], ["EA2"], ["X2"], T.X2[:]),
             lambda: tt(T.EA[:, E16(0)], ["EA0"], T.NB[:], T.EA[:, E16(5)], ["NB", "EA5"], A.mult),
+            None,
             spread,
+            lambda: claim(0, 0),
             None,
             lambda: tt(T.DL[:], ["DL"], T.FN[:], T.bk0[:, 0:C], ["FN", "bk0"], A.mult),
+            lambda: claim(0, 1),
             leave,
         ]
         for i in range(16):
-            tt(T.PR[:, i:W:16], ["PR%d" % i], T.R[:, i:W:16], T.bk4[:, 0:C], ["R", "bk4"], A.mult)
-            MM(T.bk5[:, 0:C], blk("mEX", i)[0], T.PR[:, i:W:16], False, i == 15, "bk5", ["mEX", "PR%d" % i])
+            pick(1, i)
             if i < len(chain) and chain[i] is not None:
                 chain[i]()
-        S(T.W1[:], T.bk4[:, 0:C], ["W1"], ["bk4"], scale=-1.0, bias=1.0)
+        for h, wb in enumerate(("bk3", "bk4")):
+            S(T.W1[:, 128 * h:128 * h + 128], T[wb][:, 0:128], [("W1", 128 * h, 128 * h + 128)], [wb], scale=-1.0, bias=1.0)
         if more:
             ts(T.LIM[:], ["LIM"], T.TH16[:], ["TH16", "MF"], T.MF[:], None, A.add)
         if first:
             constants_c()
 
-        V("tr", T.XT[:], ["XT"], ["bk5"], T.bk5[:, 0:C])
-        V("sc", T.S3[:], ["S3"], ["cNEG", "XT"], T.cNEG[:], T.XT[:], 0.0, A.add, A.max)
+        claim(1, 0)
+        claim(1, 1)
         if more:
             if first:
                 const_t(1)
@@ -436,14 +500,15 @@ def rank_program(g, core, T, topo):
             ts(T["D%d" % r][:], ["D%d" % r], T.KI[:], ["KI"], 4 * r, 15, SHR, AND)
         for r in range(3):
             V("cp", T.EB[:, E16(r)], ["EBd%d" % r], ["EB", "D%d" % r], T["D%d" % r][:])
-            S(T.EB[:, E16(3 + r)], T.EB[:, E16(r)], ["EBs%d" % r], ["EB", "EBd%d" % r], F.Square)
+        for r in range(3):
+            tt(T.EB[:, E16(3 + r)], ["EBs%d" % r], T["D%d" % r][:], T["D%d" % r][:], ["EB", "D%d" % r], A.mult)
+        V("tr", T.VN[:], ["VN"], ["EB", "EBz"] + ["EBd%d" % r for r in range(3)] + ["EBs%d" % r for r in range(3)], T.EB[:])
+        MM(T.bk2[:, 0:C], T.mXX[:], T.VN[:], True, True, "bk2", ["mXX", "VN"])
         if more:
             codev(t + 1, 0)
-        V("tr", T.VN[:], ["VN"], ["EB", "EBz"] + ["EBd%d" % r for r in range(3)] + ["EBs%d" % r for r in range(3)], T.EB[:])
-        MM(T.bk7[:, 0:C], T.mXX[:], T.VN[:], True, True, "bk7", ["mXX", "VN"])
         ts(T.VM[:, 0:2 * C:2], ["VM0"], T.VN[:], ["VN", ("cF", 30, 31)], col(30), None, A.mult)
         ts(T.VM[:, 1:2 * C:2], ["VM1"], T.VN[:], ["VN", ("cF", 2, 3)], col(2), None, A.mult)
-        S(T.RV[:], T.bk7[:, 0:C], ["RV"], ["bk7"], F.Copy)
+        S(T.RV[:], T.bk2[:, 0:C], ["RV"], ["bk2"], F.Copy)
         for k in range(16):
             MM(T.bk6[:, 0:16], blk("mEL", k)[0], T.VN[:, k:C:16], k == 0, False, "bk6", ["mEL", "VN"])
         if more:
@@ -453,19 +518,21 @@ def rank_program(g, core, T, topo):
         if t + 2 < RO:
             const_t(t + 2)
             const_g(t + 2)
-        banks = ["bk2", "bk3", "bk4", "bk5", "bk7"]
-        use = [0]
-        for be in (3, 2, 1, 0):
-            for a4 in range(4):
-                bank = banks[use[0] % len(banks)]
-                use[0] += 1
-                n, k = 64 * (be + 1), 4 * a4 + be
-                rows = slice(32 * a4, 32 * a4 + 32)
-                MM(T[bank][:, 0:n], T.VM[rows, 128 * be:128 * be + 128], T.RV[rows, 0:n], True, True, bank, ["VM0", "VM1", "RV"])
-                if (a4, be) in S_RED:
-                    S(T.JK[:, 0:n], T[bank][:, 0:n], ["JK", ("FL", k, k + 1)], [bank], F.Relu, accum_out=T.FL[:, k:k + 1])
+        banks = ["bk3", "bk4", "bk5", "bk7", "bk2"]
+        for j, (a4, pair) in enumerate(((0, (3, 2)), (0, (1, 0)), (1, (3, 2)), (3, (3, 2)), (2, (3, 2)), (1, (1, 0)), (2, (1, 0)), (3, (1, 0)))):
+            bank = banks[j % len(banks)]
+            rows = slice(32 * a4, 32 * a4 + 32)
+            part = []
+            for be in pair:
+                n = 64 * (be + 1)
+                c0 = 0 if be == pair[0] else 64 * (pair[0] + 1)
+                MM(T[bank][:, c0:c0 + n], T.VM[rows, 128 * be:128 * be + 128], T.RV[rows, 0:n], True, True, bank, ["VM0", "VM1", "RV"])
+                part.append((T[bank][:, c0:c0 + n], n, 4 * a4 + be))
+            for x, n, k in part:
+                if pair == (3, 2) and a4 < 3:
+                    S(T.JK[:, 0:n], x, ["JK", ("FL", k, k + 1)], [bank], F.Relu, accum_out=T.FL[:, k:k + 1])
                 else:
-                    V("rd", T.FL[:, k:k + 1], [("FL", k, k + 1)], [bank], T[bank][:, 0:n], AxisListType.X, A.max)
+                    V("rd", T.FL[:, k:k + 1], [("FL", k, k + 1)], [bank], x, AxisListType.X, A.max)
         if more:
             codev(t + 1, 2)
         for s in range(4):

@@ -21,7 +21,7 @@ for _n, _w, _d in [
     ("FI", C, "int32"), ("XI", C, "int32"), ("OFF", C, "uint16"), ("CM", C, "float32"), ("MG", C, "float32"), ("N4", C, "bfloat16"),
     ("KT", C, "float32"), ("S1", C, "float32"), ("VT", C, "float32"), ("S2", C, "float32"), ("XT", C, "float32"), ("S3", C, "float32"),
     ("WT", C, "float32"), ("W1", C, "bfloat16"), ("EA", C, "bfloat16"), ("EN", C, "bfloat16"), ("EB", C, "bfloat16"), ("VN", C, "bfloat16"),
-    ("VM", 2 * C, "bfloat16"), ("RV", C, "bfloat16"), ("JK", C, "bfloat16"), ("DL", C, "bfloat16"), ("UG", C, "bfloat16"),
+    ("VM", 2 * C, "bfloat16"), ("RV", C, "bfloat16"), ("JK", 4096, "bfloat16"), ("DL", C, "bfloat16"), ("UG", C, "bfloat16"),
     ("TAU", 16, "int32"), ("LB", 16, "float32"), ("TV", 16, "float32"), ("KV", 16, "int32"), ("NB", 16, "int32"),
     ("X1", 16, "int32"), ("X2", 16, "int32"), ("KI", 16, "int32"), ("D0", 16, "int32"), ("D1", 16, "int32"), ("D2", 16, "int32"),
     ("YM", 16, "float32"), ("OL", 16, "uint16"), ("FL", 16, "float32"), ("FB", 64, "bfloat16"),
@@ -203,8 +203,10 @@ def rank_program(g, core, T, topo):
         if t == 0:
             tt(blk("mQT", t)[0], [blk("mQT", t)[1]], blk("mPT", t)[0], T.mI[:], [blk("mPT", t)[1], "mI"], A.add)
         x = slice(128 * t, 128 * t + 128)
-        for p0, nm, bits, add in ((0, "KCa%d" % t, 4080, 0.0), (64, "KCb%d" % t, 15, 1.0 / 64)):
+        part = ((0, "KCa%d" % t, 4080, 0.0), (64, "KCb%d" % t, 15, 1.0 / 64))
+        for p0, nm, bits, add in part:
             ts(T.jKC[p0:p0 + 64, x], ["j" + nm], T.iKC[p0:p0 + 64, x], [blk("iKC", t)[1]], bits, None, AND)
+        for p0, nm, bits, add in part:
             ts(T.mKC[p0:p0 + 64, x], [nm], T.jKC[p0:p0 + 64, x], ["j" + nm], 0.25, add, A.mult, A.add)
 
     def const_g(t):
@@ -249,30 +251,40 @@ def rank_program(g, core, T, topo):
         S(T.FN[:], T.bk6[:, 0:C], ["FN"], ["bk6"], F.Relu, scale=1.0 / FLAG)
 
     codes(0)
-    for k in range(5):
-        codev(0, k)
+    V("ms", T.U[:, W:UW], [("U", W, UW)], [], -1.0)
+    V("ms", T.cMASK[:], ["cMASK"], [], 1.0)
+    codev(0, 0)
+    V("ms", T.cNEG[:], ["cNEG"], [], 0.0)
+    codev(0, 1)
+    V("ms", T.cMASK[:, E16(0)], ["cMASK"], [], 0.0)
+    V("ms", T.cNEG[:, E16(0)], ["cNEG"], [], -2.0 ** 26)
+    V("ms", T.EA[:], EAS, [], 0.0)
+    codev(0, 2)
+    V("ms", T.EB[:], ["EB"], [], 1.0)
+    V("ms", T.EA[:, E16(4)], ["EA4"], [], 1.0)
+    V("ms", T.mZ[:], ["mZ"], [], 0.0)
+    V("ms", T.mXX[:], ["mXX"], [], 0.0)
+    codev(0, 3)
+    codev(0, 4)
     allpx = ["PXP%d" % i for i in range(16)]
     for i in range(16):
         if i < 11:
             S(T.PXP[:, i:W:16], T.P[:], [allpx[i]], ["P"], F.Copy)
         else:
             V("cp", T.PXP[:, i:W:16], [allpx[i]], ["P"], T.P[:])
-    V("ms", T.U[:, W:UW], [("U", W, UW)], [], -1.0)
 
     S(T.mI16[:], T.mI[:], ["mI16"], ["mI"], F.Copy, scale=16.0)
     S(T.mP256[:], T.mI[:], ["mP256"], ["mI"], F.Copy, scale=-256.0)
     ts(T.cJ[:], ["cJ"], T.cM[:], ["cM"], 15, None, AND)
     ts(T.mCH[:], ["mCH"], T.cJ[:], ["cJ"], -1.0 / 128, 15.0 / 128, A.mult, A.add)
     ts(T.mCV[:], ["mCV"], T.cJ[:], ["cJ"], -2.0, 30.0, A.mult, A.add)
-    S(T.mIF[:], T.mI[:], ["mIF"], ["mI"], F.Copy)
+    S(T.mIF[:], T.mI[:], ["mIF"], ["mI"], F.Copy, scale=1.0 / 16)
 
     def constants_0():
         ts(T.cB[:], ["cB"], T.cJ[:], ["cJ"], 1.0, None, A.mult)
         ts(T.cT[:], ["cT"], T.cD[:], ["cD"], 256.0, None, A.is_gt)
-        V("ms", T.mZ[:], ["mZ"], [], 0.0)
         tt(T.cMI[:], ["cMI"], T.cB[:], T.cA[:], ["cB", "cA"], A.add)
         tt(T.cB[:], ["cB"], T.cT[:], T.cBM[:], ["cT", "cBM"], A.mult)
-        V("ms", T.mXX[:], ["mXX"], [], 0.0)
         for i in range(16):
             ts(blk("mE", i)[0], [blk("mE", i)[1]], T.cMI[:], ["cMI"], float(i), 4096.0, A.is_equal, A.mult)
         tt(T.mF0[:], ["mF0"], T.mI[:], T.cB[:], ["cB", "mI"], A.subtract)
@@ -284,35 +296,26 @@ def rank_program(g, core, T, topo):
             cell("mXX", 0, r, m, x)
 
     def constants_a():
-        V("ms", T.cMASK[:], ["cMASK"], [], 1.0)
-        V("ms", T.cNEG[:], ["cNEG"], [], 0.0)
-        V("ms", T.cMASK[:, E16(0)], ["cMASK"], [], 0.0)
-        V("ms", T.cNEG[:, E16(0)], ["cNEG"], [], -2.0 ** 26)
         V("cp", T.cBL[:], ["cBL"], ["cG"], T.cG[:])
         V("cp", T.THF[0:8, :], ["THF"], ["THI"], T.THI[0:8, :])
         ts(T.THQ[0:8, :], ["THQ"], T.cG[0:8, :], ["cG"], 1, None, AND)
-        ts(T.cJ[:], ["cJ"], T.cM[:], ["cM"], 5, None, SHR)
+        ts(T.cT[:], ["cT"], T.cM[:], ["cM"], 5, None, SHR)
         ts(T.TH8[0:8, :], ["TH8"], T.THQ[0:8, :], ["THQ", ("cF", 0, 8), "THF"], T.cF[0:8, 3:4], T.THF[0:8, :], A.is_equal, A.mult)
-        ts(T.mTH[0:8, :], ["mTH"], T.cJ[0:8, :], ["cJ", ("cF", 0, 8)], T.cF[0:8, 5:6], 16.0, A.is_equal, A.mult)
-        V("ms", T.EA[:], EAS, [], 0.0)
-        V("ms", T.EA[:, E16(4)], ["EA4"], [], 1.0)
+        ts(T.mTH[0:8, :], ["mTH"], T.cT[0:8, :], ["cT", ("cF", 0, 8)], T.cF[0:8, 5:6], 16.0, A.is_equal, A.mult)
         MM(T.bk6[:, 0:16], T.mTH[0:8, :], T.TH8[0:8, :], True, True, "bk6", ["mTH", "TH8"])
         V("cp", T.TH16[:], ["TH16"], ["bk6"], T.bk6[:, 0:16])
         V("cp", T.LIM[:], ["LIM"], ["bk6"], T.bk6[:, 0:16])
-        ts(T.mCX[0:64, :], ["mCX0"], T.mCV[0:64, :], ["mCV"], 32.0, None, A.mult)
-        V("ms", T.mCX[64:128, :], ["mCX1"], [], 15.0 / 128)
+        ts(T.mCX[0:64, :], ["mCX0"], T.mCV[0:64, :], ["mCV"], 2.0, None, A.mult)
+        V("ms", T.mCX[64:128, :], ["mCX1"], [], 15.0 / 2048)
 
     def constants_b():
-        S(T.mEX[:], T.mE[:], ["mEX"], ["mE"], F.Copy, scale=16.0)
         fcol(20, 1, 0.0, 1.0 / 4096, A.is_equal, A.mult)
         for r, x in ((1, 16.0), (2, 256.0), (7, 8192.0)):
             fcol(21 + r, 1, float(r), x / 4096, A.is_equal, A.mult)
         for r in (1, 2, 7):
             tt(col(20), [("cF", 20, 21)], col(20), col(21 + r), [("cF", 20, 29)], A.add)
-        S(T.mEL[:], T.mE[:], ["mEL"], ["mE", ("cF", 20, 21)], F.Copy, scale=col(20))
 
     def constants_c():
-        V("ms", T.EB[:], ["EB"], [], 1.0)
         ts(T.X1[:], ["X1"], T.cG[:], ["cG"], 1, None, SHR)
         fcol(30, 2, 0.0, None, A.is_equal)
         ts(T.EB[:, E16(6)], ["EB"], T.X1[:], ["X1", ("cF", 7, 8)], 32.0, col(7), A.mult, A.add)
@@ -379,11 +382,10 @@ def rank_program(g, core, T, topo):
             gather_v(NT * k, NT)
             gather_s(k)
             if first and k == 0:
+                constants_a()
                 constants_0()
             gains(k)
         votes(0)
-        if first:
-            constants_a()
         gather_v(128, 32)
         gather_s(2)
         level(0, 0)
@@ -408,7 +410,7 @@ def rank_program(g, core, T, topo):
             pr, xb, wb = "PR%d_%d" % (h, i), ("bk5", "bk7")[h], ("bk3", "bk4")[h]
             lo, hi = 2048 * h, 2048 * h + 2048
             tt(T.PR[:, lo + i:hi:16], [pr], T.R[:, lo + i:hi:16], T[wb][:, 0:128], [("R", lo, hi), wb], A.mult)
-            MM(T[xb][:, 0:128], blk("mEX", i)[0], T.PR[:, lo + i:hi:16], False, i == 15, xb, ["mEX", pr])
+            MM(T[xb][:, 0:128], blk("mE", i)[0], T.PR[:, lo + i:hi:16], False, i == 15, xb, [blk("mE", i)[1], pr])
 
         for h in range(2):
             xb = ("bk5", "bk7")[h]
@@ -485,6 +487,7 @@ def rank_program(g, core, T, topo):
         if more:
             ts(T.LIM[:], ["LIM"], T.TH16[:], ["TH16", "MF"], T.MF[:], None, A.add)
         if first:
+            S(T.mEL[:], T.mE[:], ["mEL"], ["mE", ("cF", 20, 21)], F.Copy, scale=col(20))
             constants_c()
 
         claim(1, 0)
@@ -494,7 +497,7 @@ def rank_program(g, core, T, topo):
                 const_t(1)
                 const_g(1)
             codes(t + 1)
-        V("cp", T.KI[:], ["KI"], ["S3"], T.S3[:, 15:C:16])
+        ts(T.KI[:], ["KI"], T.S3[:, 15:C:16], ["S3"], 16.0, None, A.mult)
         tt(T.EB[:, E16(7)], ["EBz"], T.S3[:, 15:C:16], T.LB[:], ["EB", "S3"] + LBS, A.is_lt)
         for r in range(3):
             ts(T["D%d" % r][:], ["D%d" % r], T.KI[:], ["KI"], 4 * r, 15, SHR, AND)
@@ -515,9 +518,8 @@ def rank_program(g, core, T, topo):
             codev(t + 1, 1)
         if first:
             constants_d()
-        if t + 2 < RO:
-            const_t(t + 2)
-            const_g(t + 2)
+        if more:
+            codev(t + 1, 2)
         banks = ["bk3", "bk4", "bk5", "bk7", "bk2"]
         for j, (a4, pair) in enumerate(((0, (3, 2)), (0, (1, 0)), (1, (3, 2)), (3, (3, 2)), (2, (3, 2)), (1, (1, 0)), (2, (1, 0)), (3, (1, 0)))):
             bank = banks[j % len(banks)]
@@ -530,11 +532,9 @@ def rank_program(g, core, T, topo):
                 part.append((T[bank][:, c0:c0 + n], n, 4 * a4 + be))
             for x, n, k in part:
                 if pair == (3, 2) and a4 < 3:
-                    S(T.JK[:, 0:n], x, ["JK", ("FL", k, k + 1)], [bank], F.Relu, accum_out=T.FL[:, k:k + 1])
+                    S(T.JK[:, 256 * k:256 * k + n], x, ["JK%d" % k, ("FL", k, k + 1)], [bank], F.Relu, accum_out=T.FL[:, k:k + 1])
                 else:
                     V("rd", T.FL[:, k:k + 1], [("FL", k, k + 1)], [bank], x, AxisListType.X, A.max)
-        if more:
-            codev(t + 1, 2)
         for s in range(4):
             if s < 2:
                 S(T.FB[:, s:64:4], T.FL[:], ["FB%d" % s], ["FL", ("cF", 40 + s, 41 + s)], F.Relu, scale=col(40 + s))
@@ -544,12 +544,15 @@ def rank_program(g, core, T, topo):
             MM(T.bk6[:, 0:16], blk("mLM", a4)[0], T.FB[:, 16 * a4:16 * a4 + 16], False, a4 == 3, "bk6", ["mLM"] + ["FB%d" % s for s in range(4)])
         if more:
             codev(t + 1, 3)
+            codev(t + 1, 4)
         tt(T.YM[:], ["YM"], T.cDUM[:], T.bk6[:, 0:16], ["cDUM", "bk6"], A.min)
         V("cp", T.OL[:], ["OL"], ["YM"], T.YM[:])
         S(T.UG[:], T.U[:].indirect(T.OL[:]), ["UG"], ["U", "OL"], F.Copy)
         if more:
-            codev(t + 1, 4)
             codes2(t + 1)
+        if t + 2 < RO:
+            const_t(t + 2)
+            const_g(t + 2)
         tt(T.U[:].indirect(T.OL[:]), ["U"], T.UG[:], T.W1[:], ["UG", "W1", "OL"], A.mult)
 
     S(T.OUTT[:], T["TB%d" % RO][:], ["OUTT"], ["TB%d" % RO], scale=0.5)

from concourse.mybir import AluOpType as A, AxisListType, ActivationFunctionType as F

N = 4
RO = 6
C = 256
W = 4096
UW = 4368
VOID = 4096
DUMMY = 4112
FLAG = 2.0 ** 19
BIG = 2.0 ** 25
MAGIC = 1.5 * 2.0 ** 23
CH = 4
NT = C // CH
RHO = [(5 * t) % 16 for t in range(RO)]

SCRATCH = {}
for _n, _w, _d in [
    ("U", UW, "bfloat16"), ("PXP", W, "bfloat16"), ("R", W, "bfloat16"), ("M", W, "bfloat16"), ("PR", W, "bfloat16"),
    ("P", C, "bfloat16"), ("TI", C, "int32"), ("NF", C, "bfloat16"), ("FN", C, "bfloat16"), ("QF", C, "float32"),
    ("FI", C, "int32"), ("XI", C, "int32"), ("OFF", C, "uint16"), ("CM", C, "float32"), ("MG", C, "float32"), ("N4", C, "bfloat16"),
    ("KT", C, "float32"), ("S1", C, "float32"), ("VT", C, "float32"), ("S2", C, "float32"), ("XT", C, "float32"), ("S3", C, "float32"),
    ("WT", C, "float32"), ("W1", C, "bfloat16"), ("EA", C, "bfloat16"), ("EN", C, "bfloat16"), ("EB", C, "bfloat16"), ("VN", C, "bfloat16"),
    ("VM", 2 * C, "bfloat16"), ("RV", C, "bfloat16"), ("JK", 4096, "bfloat16"), ("DL", C, "bfloat16"), ("UG", C, "bfloat16"),
    ("TAU", 16, "int32"), ("LB", 16, "float32"), ("TV", 16, "float32"), ("KV", 16, "int32"), ("NB", 16, "int32"),
    ("X1", 16, "int32"), ("X2", 16, "int32"), ("KI", 16, "int32"), ("D0", 16, "int32"), ("D1", 16, "int32"), ("D2", 16, "int32"),
    ("YM", 16, "float32"), ("OL", 16, "uint16"), ("FL", 16, "float32"), ("FB", 64, "bfloat16"),
    ("LIM", 16, "float32"), ("TH16", 16, "float32"), ("THI", 1, "int32"), ("THF", 1, "float32"), ("TH8", 16, "float32"), ("THQ", 16, "int32"),
    ("MC", 1, "float32"), ("MA", 1, "float32"), ("MQ", 1, "float32"), ("MR", 1, "float32"), ("MF", 1, "float32"), ("MJK", 16, "float32"),
    ("OUTT", C, "float32"), ("OUTC", C, "float32"), ("TS", C * RO, "bfloat16"),
    ("cM", 128, "int32"), ("cD", 128, "int32"), ("cJ", 128, "int32"), ("cT", 128, "int32"), ("cG", 16, "int32"),
    ("cP", 1, "int32"), ("cI", 8, "int32"), ("cF", 64, "float32"), ("cBM", 128, "bfloat16"), ("cMI", 128, "bfloat16"), ("cDD", 128, "bfloat16"),
    ("cA", 128, "bfloat16"), ("cB", 128, "bfloat16"), ("mI", 128, "bfloat16"), ("mI16", 128, "bfloat16"), ("mP256", 128, "bfloat16"), ("mIF", 128, "float32"),
    ("mPT", 128 * RO, "bfloat16"), ("mQT", 128 * RO, "bfloat16"), ("mKC", 128 * RO, "bfloat16"), ("iKC", 128 * RO, "int32"), ("jKC", 128 * RO, "int32"),
    ("mE", 2048, "bfloat16"), ("mEX", 2048, "bfloat16"), ("mEL", 2048, "bfloat16"), ("mCH", 128, "bfloat16"), ("mCV", 128, "bfloat16"), ("mCX", 128, "bfloat16"),
    ("mF0", 128, "bfloat16"), ("mFN", 128 * RO, "bfloat16"), ("mBR", 128 * RO, "bfloat16"), ("mNR", 128 * RO, "bfloat16"), ("mB0", 128, "bfloat16"), ("mON", C, "bfloat16"),
    ("mXX", 128, "bfloat16"), ("mZ", 128, "bfloat16"), ("mLM", 512, "bfloat16"), ("mTH", 128, "float32"),
    ("cMASK", C, "float32"), ("cNEG", C, "float32"), ("cBL", 16, "uint16"), ("cDUM", 16, "float32"),
]:
    SCRATCH[_n] = ("sbuf", [128, _w], _d)
for _t in range(RO + 1):
    SCRATCH["TB%d" % _t] = ("sbuf", [128, C], "bfloat16")
for _b in range(8):
    SCRATCH["bk%d" % _b] = ("psum", [128, 512], "float32")
SEMAPHORES = ["v", "s", "p", "g", "snd"] + ["arr%d" % t for t in range(1, RO + 1)] + ["dma%d" % k for k in range(6)]
AND, SHR = A.bitwise_and, A.arith_shift_right


def rank_program(g, core, T, topo):
    rank = T.rank_of(core)
    if rank is None:
        return
    queue = {"v": g.vector, "s": g.scalar, "p": g.tensor, "g": g, "y": g.sync}
    count = {}
    known = {q: {} for q in queue}
    done = {}
    last = {}

    def need(q, sem, val):
        if known[q].get(sem, 0) >= val:
            return
        queue[q].wait_ge(T.sem[sem], val)
        known[q][sem] = val
        for k, x in done.get((sem, val), {}).items():
            if known[q].get(k, 0) < x:
                known[q][k] = x

    def spans(views):
        return [(x, 0, 1 << 20) if isinstance(x, str) else x for x in views]

    def order(q, reads, writes):
        todo = {}
        reads, writes = spans(reads), spans(writes)
        for views, wr in ((reads, False), (writes, True)):
            for b, lo, hi in views:
                for l2, h2, w2, q2, s2, v2 in last.get(b, []):
                    if b.startswith("bk"):
                        hit = q2 != q or (w2 and q != "p")
                    else:
                        hit = (wr or w2) and l2 < hi and lo < h2
                    if hit and todo.get(s2, 0) < v2:
                        todo[s2] = v2
        for s2, v2 in sorted(todo.items(), key=lambda kv: -sum(done.get(kv, {}).values())):
            need(q, s2, v2)
        return reads, writes

    def note(q, reads, writes, sem, val):
        for views, wr in ((reads, False), (writes, True)):
            for b, lo, hi in views:
                keep = []
                for e in last.get(b, []):
                    if b.startswith("bk"):
                        if e[3] != q or wr or not e[2]:
                            continue
                    elif wr and lo <= e[0] and e[1] <= hi:
                        continue
                    elif not wr and not e[2] and e[3] == q and lo <= e[0] and e[1] <= hi:
                        continue
                    keep.append(e)
                keep.append((lo, hi, wr, q, sem, val))
                last[b] = keep
        know = dict(known[q])
        know[sem] = val
        done[(sem, val)] = know

    def run(q, call, reads, writes):
        reads, writes = order(q, reads, writes)
        call(queue[q]).then_inc(T.sem[q], 1)
        count[q] = count.get(q, 0) + 1
        note(q, reads, writes, q, count[q])

    def dma(q, k, out, in_, reads, writes):
        sem = "dma%d" % k
        reads, writes = order(q, reads, writes)
        queue[q].dma_start(out, in_).then_inc(T.sem[sem], 16)
        note(q, reads, writes, sem, 16)

    def V(name, out, wr, rd, *a, **k):
        run("v", lambda e: {"tt": e.tensor_tensor, "ts": e.tensor_scalar, "cp": e.tensor_copy, "tr": e.transpose, "sc": e.tensor_tensor_scan,
                            "rd": e.tensor_reduce, "ms": e.memset}[name](out, *a, **k), rd, wr)

    def S(out, in_, wr, rd, func=F.Identity, **k):
        run("s", lambda e: e.activation(out, in_, func, **k), rd, wr)

    def MM(out, lhsT, rhs, start, stop, bank, rd):
        run("p", lambda e: e.matmul(out, lhsT, rhs, start, stop), rd, [bank])

    def ts(out, wr, in0, rd, s1, s2, op0, op1=None):
        if op1 is None:
            V("ts", out, wr, rd, in0, s1, None, op0)
        else:
            V("ts", out, wr, rd, in0, s1, s2, op0, op1)

    def tt(out, wr, a, b, rd, op):
        V("tt", out, wr, rd, a, b, op)

    def iota(out, wr, pattern, base, cm):
        run("g", lambda e: e.iota(out, pattern, base, cm), [], [wr])

    def fill(name, c0, pattern, base, cm, value, src=None, s0=0):
        n = 1
        for p in pattern:
            n *= p[1]
        if src is None:
            src, s0 = name, c0
        run("g", lambda e: e.affine_select(T[name][:, c0:c0 + n], T[src][:, s0:s0 + n], pattern, A.not_equal, value, base, cm),
            [(src, s0, s0 + n)], [(name, c0, c0 + n)])

    def cell(name, c0, row, column, value, src=None, s0=0):
        fill(name, c0, [[-16, 8], [1000, 16]], -row - 1000 * column, 1, value, src, s0)

    def col(k):
        return T.cF[:, k:k + 1]

    def fcol(k, src, s1, s2, op0, op1=None):
        ts(col(k), [("cF", k, k + 1)], col(src), [("cF", src, src + 1)], s1, s2, op0, op1)

    def icol(k, s1, s2, op0, op1=None):
        ts(T.cI[:, k:k + 1], [("cI", k, k + 1)], T.cP[:], ["cP"], s1, s2, op0, op1)

    EAS = ["EA%d" % r for r in range(6)]
    E16 = lambda r: slice(r, C, 16)
    blk = lambda name, k: (T[name][:, 128 * k:128 * k + 128], (name, 128 * k, 128 * k + 128))

    dma("y", 0, T.TI[:], T.tst[:], [], ["TI"])
    dma("s", 1, T.P[:], T.pr[:], [], ["P"])
    dma("y", 3, T.U[:, 0:W], T.cov[:], [], [("U", 0, W)])
    dma("s", 2, T.THI[0:8, :], T.th[:], [], ["THI"])

    iota(T.cD[:], "cD", [[1, 128]], 256, -1)
    iota(T.cM[:], "cM", [[1, 128]], 0, 0)
    iota(T.cP[:], "cP", [[0, 1]], 0, 1)
    V("ms", T.mON[:], ["mON"], [], 1.0)
    for k, x in ((60, -511.0 * FLAG), (61, MAGIC), (62, -MAGIC), (63, -127.5), (59, BIG)):
        V("ms", T.cF[:, k:k + 1], [("cF", k, k + 1)], [], x)

    def icodes(t):
        iota(blk("iKC", t)[0], blk("iKC", t)[1], [[0, 8], [613, 16]], 77 * t, 0)
    icodes(0)
    iota(T.cG[:], "cG", [[1, 16]], 0, 0)
    icol(0, 4, None, SHR)
    icol(1, 15, None, AND)
    icol(2, 4, 1, SHR, AND)
    icol(3, 1, None, AND)
    icol(4, 31, 1, AND, SHR)
    icol(5, 1, None, SHR)
    icol(6, 5, None, SHR)
    icol(7, 31, None, AND)
    V("cp", T.cF[:, 0:8], [("cF", 0, 8)], ["cI"], T.cI[:])
    ts(T.cJ[:], ["cJ"], T.cM[:], ["cM"], 4, None, SHR)
    ts(T.cT[:], ["cT"], T.cD[:], ["cD"], 15, None, AND)
    ts(T.cBM[:], ["cBM"], T.cJ[:], ["cJ", ("cF", 0, 1)], col(0), None, A.is_equal)
    ts(T.cB[:], ["cB"], T.cT[:], ["cT"], 1.0, None, A.mult)
    ts(T.cA[:], ["cA"], T.cBM[:], ["cBM"], -100.0, 100.0, A.mult, A.add)
    tt(T.cDD[:], ["cDD"], T.cB[:], T.cA[:], ["cA", "cB"], A.add)

    def eqm(name, k, val, scale):
        ts(blk(name, k)[0], [blk(name, k)[1]], T.cDD[:], ["cDD"], float(val), float(scale), A.is_equal, A.mult)
    eqm("mI", 0, 0, 1)

    def const_t(t):
        eqm("mPT", t, (-(1 + t)) % 16, 1)
        if t == 0:
            tt(blk("mQT", t)[0], [blk("mQT", t)[1]], blk("mPT", t)[0], T.mI[:], [blk("mPT", t)[1], "mI"], A.add)
        x = slice(128 * t, 128 * t + 128)
        part = ((0, "KCa%d" % t, 4080, 0.0), (64, "KCb%d" % t, 15, 1.0 / 64))
        for p0, nm, bits, add in part:
            ts(T.jKC[p0:p0 + 64, x], ["j" + nm], T.iKC[p0:p0 + 64, x], [blk("iKC", t)[1]], bits, None, AND)
        for p0, nm, bits, add in part:
            ts(T.mKC[p0:p0 + 64, x], [nm], T.jKC[p0:p0 + 64, x], ["j" + nm], 0.25, add, A.mult, A.add)

    def const_g(t):
        rho = RHO[t]
        if t:
            fill("mQT", 128 * t, [[-1, 128]], 0, 1, 1.0, "mPT", 128 * t)
        fill("mFN", 128 * t, [[0, 8], [1, 16]], -rho, 0, 0.0, "mF0", 0)
        cell("mNR", 128 * t, rho, rho, 0.0, "mI", 0)
        for k, (r, x) in enumerate(((1, -32.0), (2, 2.0), (3, 32.0), (4, 480.0))):
            if k == 0:
                cell("mBR", 128 * t, r, rho, x, "mZ", 0)
            else:
                cell("mBR", 128 * t, r, rho, x)
    const_t(0)
    ts(T.TB0[:], ["TB0"], T.TI[:], ["TI"], 2.0, None, A.mult)

    def codes(t):
        TB = "TB%d" % t
        tb = T[TB]
        S(T.NF[:], tb[:], ["NF"], [TB, ("cF", 59, 64)], F.Relu, scale=FLAG, bias=col(60))
        MM(T.bk0[:, 0:C], blk("mPT", t)[0], tb[:], True, True, "bk0", [blk("mPT", t)[1], TB])
        MM(T.bk1[:, 0:C], blk("mKC", t)[0], T.mON[:], True, False, "bk1", ["KCa%d" % t, "KCb%d" % t, "mON"])
        MM(T.bk1[:, 0:C], blk("mQT", t)[0], tb[:], False, False, "bk1", [blk("mQT", t)[1], TB])
        MM(T.bk1[:, 0:C], blk("mQT", t)[0], T.NF[:], False, True, "bk1", [blk("mQT", t)[1], "NF"])

    def codev(t, k):
        if k == 0:
            tt(T.QF[:], ["QF"], T["TB%d" % t][:], T.bk0[:, 0:C], ["TB%d" % t, "bk0"], A.mult)
        elif k == 1:
            tt(T.FI[:], ["FI"], T.QF[:], T.bk1[:, 0:C], ["QF", "bk1"], A.add)
        elif k == 2:
            ts(T.XI[:], ["XI"], T.FI[:], ["FI"], 4, 0x7FFF8FFF, SHR, AND)
        elif k == 3:
            ts(T.OFF[:], ["OFF"], T.XI[:], ["XI"], float(VOID), None, A.min)
        else:
            ts(T.CM[:], ["CM"], T.XI[:], ["XI"], float(VOID - 1), -7.5, A.min, A.add)

    def codes2(t):
        S(T.MG[:], T.CM[:], ["MG"], ["CM", ("cF", 59, 64)], scale=1.0 / 16, bias=col(61))
        S(T.N4[:], T.MG[:], ["N4"], ["MG", ("cF", 59, 64)], bias=col(62))
        MM(T.bk6[:, 0:C], blk("mFN", t)[0], T.NF[:], True, True, "bk6", [blk("mFN", t)[1], "NF"])
        S(T.FN[:], T.bk6[:, 0:C], ["FN"], ["bk6"], F.Relu, scale=1.0 / FLAG)

    codes(0)
    V("ms", T.U[:, W:UW], [("U", W, UW)], [], -1.0)
    V("ms", T.cMASK[:], ["cMASK"], [], 1.0)
    codev(0, 0)
    V("ms", T.cNEG[:], ["cNEG"], [], 0.0)
    codev(0, 1)
    V("ms", T.cMASK[:, E16(0)], ["cMASK"], [], 0.0)
    V("ms", T.cNEG[:, E16(0)], ["cNEG"], [], -2.0 ** 26)
    V("ms", T.EA[:], EAS, [], 0.0)
    codev(0, 2)
    V("ms", T.EB[:], ["EB"], [], 1.0)
    V("ms", T.EA[:, E16(4)], ["EA4"], [], 1.0)
    V("ms", T.mZ[:], ["mZ"], [], 0.0)
    V("ms", T.mXX[:], ["mXX"], [], 0.0)
    codev(0, 3)
    codev(0, 4)
    allpx = ["PXP%d" % i for i in range(16)]
    for i in range(16):
        if i < 11:
            S(T.PXP[:, i:W:16], T.P[:], [allpx[i]], ["P"], F.Copy)
        else:
            V("cp", T.PXP[:, i:W:16], [allpx[i]], ["P"], T.P[:])

    S(T.mI16[:], T.mI[:], ["mI16"], ["mI"], F.Copy, scale=16.0)
    S(T.mP256[:], T.mI[:], ["mP256"], ["mI"], F.Copy, scale=-256.0)
    ts(T.cJ[:], ["cJ"], T.cM[:], ["cM"], 15, None, AND)
    ts(T.mCH[:], ["mCH"], T.cJ[:], ["cJ"], -1.0 / 128, 15.0 / 128, A.mult, A.add)
    ts(T.mCV[:], ["mCV"], T.cJ[:], ["cJ"], -2.0, 30.0, A.mult, A.add)
    S(T.mIF[:], T.mI[:], ["mIF"], ["mI"], F.Copy, scale=1.0 / 16)

    def constants_0():
        ts(T.cB[:], ["cB"], T.cJ[:], ["cJ"], 1.0, None, A.mult)
        ts(T.cT[:], ["cT"], T.cD[:], ["cD"], 256.0, None, A.is_gt)
        tt(T.cMI[:], ["cMI"], T.cB[:], T.cA[:], ["cB", "cA"], A.add)
        tt(T.cB[:], ["cB"], T.cT[:], T.cBM[:], ["cT", "cBM"], A.mult)
        for i in range(16):
            ts(blk("mE", i)[0], [blk("mE", i)[1]], T.cMI[:], ["cMI"], float(i), 4096.0, A.is_equal, A.mult)
        tt(T.mF0[:], ["mF0"], T.mI[:], T.cB[:], ["cB", "mI"], A.subtract)
        const_g(0)
        fill("mB0", 0, [[-16, 8], [0, 16]], 0, 1, 2.0, "mZ", 0)
        fill("mB0", 0, [[-16, 8], [0, 16]], -5, 1, -512.0)
        for r, m, x in [(k, k, 512.0) for k in range(3)] + [(3 + k, 8 + k, -256.0) for k in range(3)] + [(8 + k, 3 + k, -256.0) for k in range(3)] + \
                [(6, 11, -1.0), (11, 6, 1.0), (7, 12, -16384.0)]:
            cell("mXX", 0, r, m, x)

    def constants_a():
        V("cp", T.cBL[:], ["cBL"], ["cG"], T.cG[:])
        V("cp", T.THF[0:8, :], ["THF"], ["THI"], T.THI[0:8, :])
        ts(T.THQ[0:8, :], ["THQ"], T.cG[0:8, :], ["cG"], 1, None, AND)
        ts(T.cT[:], ["cT"], T.cM[:], ["cM"], 5, None, SHR)
        ts(T.TH8[0:8, :], ["TH8"], T.THQ[0:8, :], ["THQ", ("cF", 0, 8), "THF"], T.cF[0:8, 3:4], T.THF[0:8, :], A.is_equal, A.mult)
        ts(T.mTH[0:8, :], ["mTH"], T.cT[0:8, :], ["cT", ("cF", 0, 8)], T.cF[0:8, 5:6], 16.0, A.is_equal, A.mult)
        MM(T.bk6[:, 0:16], T.mTH[0:8, :], T.TH8[0:8, :], True, True, "bk6", ["mTH", "TH8"])
        V("cp", T.TH16[:], ["TH16"], ["bk6"], T.bk6[:, 0:16])
        V("cp", T.LIM[:], ["LIM"], ["bk6"], T.bk6[:, 0:16])
        ts(T.mCX[0:64, :], ["mCX0"], T.mCV[0:64, :], ["mCV"], 2.0, None, A.mult)
        V("ms", T.mCX[64:128, :], ["mCX1"], [], 15.0 / 2048)

    def constants_b():
        fcol(20, 1, 0.0, 1.0 / 4096, A.is_equal, A.mult)
        for r, x in ((1, 16.0), (2, 256.0), (7, 8192.0)):
            fcol(21 + r, 1, float(r), x / 4096, A.is_equal, A.mult)
        for r in (1, 2, 7):
            tt(col(20), [("cF", 20, 21)], col(20), col(21 + r), [("cF", 20, 29)], A.add)

    def constants_c():
        ts(T.X1[:], ["X1"], T.cG[:], ["cG"], 1, None, SHR)
        fcol(30, 2, 0.0, None, A.is_equal)
        ts(T.EB[:, E16(6)], ["EB"], T.X1[:], ["X1", ("cF", 7, 8)], 32.0, col(7), A.mult, A.add)
        ts(T.cDUM[:], ["cDUM"], T.cG[:], ["cG", ("cF", 1, 2)], 16.0, col(1), A.mult, A.add)
        fcol(33, 3, 16.0, col(4), A.mult, A.add)

    def constants_d():
        ts(T.cDUM[:], ["cDUM"], T.cDUM[:], ["cDUM"], float(DUMMY), None, A.add)
        for a in range(1, 4):
            fcol(33 + a, 33, 32.0 * a, None, A.add)
        for s in range(4):
            fcol(40 + s, 6, float(s), None, A.is_equal)
        for a in range(4):
            ts(blk("mLM", a)[0], [blk("mLM", a)[1]], T.cM[:], ["cM", ("cF", 33 + a, 34 + a)], col(33 + a), 8192.0, A.is_equal, A.mult)

    def votes(k):
        lo, hi = 1024 * k, 1024 * k + 1024
        for i in range(16):
            MM(T.bk2[:, NT * k:NT * (k + 1)], blk("mE", i)[0], T.R[:, lo + i:hi:16], False, False, "bk2", [blk("mE", i)[1], ("R", lo, hi)])

    for t in range(RO):
        first, more = t == 0, t < RO - 1
        TB = "TB%d" % t
        LBS = ["LB00", "LB10", "LB01", "LB11"]
        l3 = T.EA[:, E16(3)]

        def gather_v(c0, n):
            lo, hi = 16 * c0, 16 * (c0 + n)
            tt(T.M[:, lo:hi], [("M", lo, hi)], T.U[:].indirect(T.OFF[:, c0:c0 + n]), T.PXP[:, lo:hi], ["U", ("OFF", c0, c0 + n)] + allpx, A.max)

        def gather_s(k):
            lo, hi = 1024 * k, 1024 * k + 1024
            S(T.R[:, lo:hi], T.U[:].indirect(T.OFF[:, NT * k:NT * k + NT]), [("R", lo, hi)], ["U", ("OFF", NT * k, NT * k + NT)], F.Copy)

        def gains(k):
            lo, hi, bank, c0 = 1024 * k, 1024 * k + 1024, ("bk0", "bk1")[k // 2], NT * (k % 2)
            for i in range(16):
                MM(T[bank][:, c0:c0 + NT], T.mI16[:], T.M[:, lo + i:hi:16], False, k % 2 == 1 and i == 15, bank, ["mI16", ("M", lo, hi)])

        def level(h, step):
            a, b, a8 = 128 * h, 128 * h + 128, 8 * h
            kt, s1, tau, wt = ("KT", a, b), ("S1", a, b), ("TAU", a8, a8 + 8), ("WT", a, b)
            gb, wb = ("bk0", "bk1")[h], ("bk3", "bk4")[h]
            if step == 0:
                V("tr", T.KT[:, a:b], [kt], [gb], T[gb][:, 0:128])
            elif step == 1:
                V("sc", T.S1[:, a:b], [s1], ["cMASK", kt], T.cMASK[:, 0:128], T.KT[:, a:b], 0.0, A.mult, A.max)
            elif step == 2:
                for gm in range(2):
                    ts(T.LB[:, a8 + gm:a8 + 8:2], ["LB%d%d" % (gm, h)], T.S1[:, a + 15 + 16 * gm:b:32], [s1, "LIM"], T.LIM[:, gm:gm + 1], BIG, A.is_lt, A.mult)
            elif step == 3:
                tt(T.TAU[:, a8:a8 + 8], [tau], T.LB[:, a8:a8 + 8], T.S1[:, a + 15:b:16], ["LB0%d" % h, "LB1%d" % h, s1], A.max)
            elif step == 4:
                tt(T.WT[:, a:b], [wt], T.TAU[:, a8:a8 + 8].indirect(T.cBL[:, 0:8]), T.KT[:, a:b], [tau, "cBL", kt], A.is_le)
            else:
                V("tr", T[wb][:, 0:128], [wb], [wt], T.WT[:, a:b])

        for h in range(2):
            gb = ("bk0", "bk1")[h]
            MM(T[gb][:, 0:128], T.mCH[:], T.mON[:, 0:128], True, False, gb, ["mCH", "mON"])
            MM(T[gb][:, 0:128], T.mP256[:], T.P[:, 128 * h:128 * h + 128], False, False, gb, ["mP256", "P"])
        MM(T.bk2[:, 0:C], T.mCV[:], T.mON[:], True, False, "bk2", ["mCV", "mON"])
        for k in range(2):
            gather_v(NT * k, NT)
            gather_s(k)
            if first and k == 0:
                constants_a()
                constants_0()
            gains(k)
        votes(0)
        gather_v(128, 32)
        gather_s(2)
        level(0, 0)
        gather_v(160, 32)
        gains(2)
        votes(1)
        level(0, 1)
        gather_s(3)
        for k in range(4):
            gather_v(192 + 16 * k, 16)
            level(0, 2 + k)
        gains(3)
        votes(2)
        if first:
            codes2(0)
        votes(3)
        MM(T.bk2[:, 0:C], T.mI[:], T.N4[:], False, True, "bk2", ["mI", "N4"])
        if first:
            constants_b()

        def pick(h, i):
            pr, xb, wb = "PR%d_%d" % (h, i), ("bk5", "bk7")[h], ("bk3", "bk4")[h]
            lo, hi = 2048 * h, 2048 * h + 2048
            tt(T.PR[:, lo + i:hi:16], [pr], T.R[:, lo + i:hi:16], T[wb][:, 0:128], [("R", lo, hi), wb], A.mult)
            MM(T[xb][:, 0:128], blk("mE", i)[0], T.PR[:, lo + i:hi:16], False, i == 15, xb, [blk("mE", i)[1], pr])

        for h in range(2):
            xb = ("bk5", "bk7")[h]
            MM(T[xb][:, 0:128], T.mIF[:], T.CM[:, 128 * h:128 * h + 128], True, False, xb, ["mIF", "CM"])
            MM(T[xb][:, 0:128], T.mCX[:], T.mON[:, 0:128], False, False, xb, ["mCX0", "mCX1", "mON"])
        vote = {
            9: lambda: ts(T.X1[:], ["X1"], T.TAU[:], ["TAU"], 15, None, AND),
            10: lambda: V("tr", T.VT[:], ["VT"], ["bk2"], T.bk2[:, 0:C]),
            12: lambda: V("sc", T.S2[:], ["S2"], ["cNEG", "VT"], T.cNEG[:], T.VT[:], 0.0, A.add, A.max),
            13: lambda: ts(T.X2[:], ["X2"], T.TAU[:], ["TAU"], 4, 15, SHR, AND),
            14: lambda: V("cp", T.KV[:], ["KV"], ["S2"], T.S2[:, 15:C:16]),
            15: lambda: ts(T.NB[:], ["NB"], T.KV[:], ["KV"], 255, None, AND),
        }
        for i in range(16):
            pick(0, i)
            if i % 2 == 1 and i < 12:
                level(1, i // 2)
                if i // 2 == 2:
                    S(T.TV[:], T.LB[:], ["TV"], LBS + [("cF", 59, 64)], scale=-1.0, bias=col(59))
                    S(l3, T.LB[:], ["EA3"], LBS, F.Sign)
            if i in vote:
                vote[i]()
        if more:
            MM(T.bk6[:, 0:16], T.mON[:, 0:128], l3, True, True, "bk6", ["mON", "EA3"])
            S(T.MJK[:], T.bk6[:, 0:16], ["MJK", "MC"], ["bk6"], scale=16.0, accum_out=T.MC[:])
            S(T.MA[:], T.MC[:], ["MA"], ["MC", ("cF", 59, 64)], scale=1.0 / 16, bias=col(63))
            S(T.MQ[:], T.MA[:], ["MQ"], ["MA", ("cF", 59, 64)], scale=1.0 / 256, bias=col(61))
            S(T.MR[:], T.MQ[:], ["MR"], ["MQ", ("cF", 59, 64)], bias=col(62))
            S(T.MF[:], T.MR[:], ["MF"], ["MR", "MC"], scale=-4096.0, bias=T.MC[:])

        def claim(h, step):
            x, s3, xb = ("XT", 128 * h, 128 * h + 128), ("S3", 128 * h, 128 * h + 128), ("bk5", "bk7")[h]
            if step == 0:
                V("tr", T.XT[:, x[1]:x[2]], [x], [xb], T[xb][:, 0:128])
            else:
                V("sc", T.S3[:, x[1]:x[2]], [s3], ["cNEG", x], T.cNEG[:, 0:128], T.XT[:, x[1]:x[2]], 0.0, A.add, A.max)
        a, b = C * t, C * t + C

        def spread():
            V("tr", T.EN[:], ["EN"], EAS, T.EA[:])
            MM(T.bk0[:, 0:C], T.mB0[:], T.EN[:], True, True, "bk0", ["mB0", "EN"])
            MM(T.bk1[:, 0:C], blk("mNR", t)[0], T[TB][:], True, False, "bk1", [blk("mNR", t)[1], TB])
            MM(T.bk1[:, 0:C], blk("mBR", t)[0], T.EN[:], False, True, "bk1", [blk("mBR", t)[1], "EN"])

        def leave():
            tt(T.TS[:, a:b], [("TS", a, b)], T.DL[:], T.bk1[:, 0:C], ["DL", "bk1"], A.add)
            step = 1 if more else -(RO - 1)
            dst, src = T.cores[(rank + step) % N], T.cores[(rank - step) % N]
            rid, pid, _se = topo.addr(dst)
            order("g", [("TS", a, b)], [])
            g.remote_dma(T["TB%d" % (t + 1)][:], T.TS[:, a:b], T.sem["arr%d" % (t + 1)], T.sem["snd"], pid, rid, topo.mask(core, dst))
            last["TB%d" % (t + 1)] = [(0, 1 << 20, True, "r", "arr%d" % (t + 1), len(topo.engines(src, core)))]
            for u in range(1 if first else t + 2, min(t + 3, RO)):
                icodes(u)
        chain = [
            lambda: tt(T.EA[:, E16(5)], ["EA5"], T.S2[:, 15:C:16], T.TV[:], ["S2", "TV"], A.is_ge),
            lambda: V("cp", T.EA[:, E16(1)], ["EA1"], ["X1"], T.X1[:]),
            lambda: V("cp", T.EA[:, E16(2)], ["EA2"], ["X2"], T.X2[:]),
            lambda: tt(T.EA[:, E16(0)], ["EA0"], T.NB[:], T.EA[:, E16(5)], ["NB", "EA5"], A.mult),
            None,
            spread,
            lambda: claim(0, 0),
            None,
            lambda: tt(T.DL[:], ["DL"], T.FN[:], T.bk0[:, 0:C], ["FN", "bk0"], A.mult),
            lambda: claim(0, 1),
            leave,
        ]
        for i in range(16):
            pick(1, i)
            if i < len(chain) and chain[i] is not None:
                chain[i]()
        for h, wb in enumerate(("bk3", "bk4")):
            S(T.W1[:, 128 * h:128 * h + 128], T[wb][:, 0:128], [("W1", 128 * h, 128 * h + 128)], [wb], scale=-1.0, bias=1.0)
        if more:
            ts(T.LIM[:], ["LIM"], T.TH16[:], ["TH16", "MF"], T.MF[:], None, A.add)
        if first:
            S(T.mEL[:], T.mE[:], ["mEL"], ["mE", ("cF", 20, 21)], F.Copy, scale=col(20))
            constants_c()

        claim(1, 0)
        claim(1, 1)
        if more:
            if first:
                const_t(1)
                const_g(1)
            codes(t + 1)
        ts(T.KI[:], ["KI"], T.S3[:, 15:C:16], ["S3"], 16.0, None, A.mult)
        tt(T.EB[:, E16(7)], ["EBz"], T.S3[:, 15:C:16], T.LB[:], ["EB", "S3"] + LBS, A.is_lt)
        for r in range(3):
            ts(T["D%d" % r][:], ["D%d" % r], T.KI[:], ["KI"], 4 * r, 15, SHR, AND)
        for r in range(3):
            V("cp", T.EB[:, E16(r)], ["EBd%d" % r], ["EB", "D%d" % r], T["D%d" % r][:])
        for r in range(3):
            tt(T.EB[:, E16(3 + r)], ["EBs%d" % r], T["D%d" % r][:], T["D%d" % r][:], ["EB", "D%d" % r], A.mult)
        V("tr", T.VN[:], ["VN"], ["EB", "EBz"] + ["EBd%d" % r for r in range(3)] + ["EBs%d" % r for r in range(3)], T.EB[:])
        MM(T.bk2[:, 0:C], T.mXX[:], T.VN[:], True, True, "bk2", ["mXX", "VN"])
        if more:
            codev(t + 1, 0)
        ts(T.VM[:, 0:2 * C:2], ["VM0"], T.VN[:], ["VN", ("cF", 30, 31)], col(30), None, A.mult)
        ts(T.VM[:, 1:2 * C:2], ["VM1"], T.VN[:], ["VN", ("cF", 2, 3)], col(2), None, A.mult)
        S(T.RV[:], T.bk2[:, 0:C], ["RV"], ["bk2"], F.Copy)
        for k in range(16):
            MM(T.bk6[:, 0:16], blk("mEL", k)[0], T.VN[:, k:C:16], k == 0, False, "bk6", ["mEL", "VN"])
        if more:
            codev(t + 1, 1)
        if first:
            constants_d()
        if more:
            codev(t + 1, 2)
        banks = ["bk3", "bk4", "bk5", "bk7", "bk2"]
        for j, (a4, pair) in enumerate(((0, (3, 2)), (0, (1, 0)), (1, (3, 2)), (3, (3, 2)), (2, (3, 2)), (1, (1, 0)), (2, (1, 0)), (3, (1, 0)))):
            bank = banks[j % len(banks)]
            rows = slice(32 * a4, 32 * a4 + 32)
            part = []
            for be in pair:
                n = 64 * (be + 1)
                c0 = 0 if be == pair[0] else 64 * (pair[0] + 1)
                MM(T[bank][:, c0:c0 + n], T.VM[rows, 128 * be:128 * be + 128], T.RV[rows, 0:n], True, True, bank, ["VM0", "VM1", "RV"])
                part.append((T[bank][:, c0:c0 + n], n, 4 * a4 + be))
            for x, n, k in part:
                if pair == (3, 2) and a4 < 3:
                    S(T.JK[:, 256 * k:256 * k + n], x, ["JK%d" % k, ("FL", k, k + 1)], [bank], F.Relu, accum_out=T.FL[:, k:k + 1])
                else:
                    V("rd", T.FL[:, k:k + 1], [("FL", k, k + 1)], [bank], x, AxisListType.X, A.max)
        for s in range(4):
            if s < 2:
                S(T.FB[:, s:64:4], T.FL[:], ["FB%d" % s], ["FL", ("cF", 40 + s, 41 + s)], F.Relu, scale=col(40 + s))
            else:
                ts(T.FB[:, s:64:4], ["FB%d" % s], T.FL[:], ["FL", ("cF", 40 + s, 41 + s)], 0.0, col(40 + s), A.is_gt, A.mult)
        for a4 in range(4):
            MM(T.bk6[:, 0:16], blk("mLM", a4)[0], T.FB[:, 16 * a4:16 * a4 + 16], False, a4 == 3, "bk6", ["mLM"] + ["FB%d" % s for s in range(4)])
        if more:
            codev(t + 1, 3)
            codev(t + 1, 4)
        tt(T.YM[:], ["YM"], T.cDUM[:], T.bk6[:, 0:16], ["cDUM", "bk6"], A.min)
        V("cp", T.OL[:], ["OL"], ["YM"], T.YM[:])
        S(T.UG[:], T.U[:].indirect(T.OL[:]), ["UG"], ["U", "OL"], F.Copy)
        if more:
            codes2(t + 1)
        if t + 2 < RO:
            const_t(t + 2)
            const_g(t + 2)
        tt(T.U[:].indirect(T.OL[:]), ["U"], T.UG[:], T.W1[:], ["UG", "W1", "OL"], A.mult)

    S(T.OUTT[:], T["TB%d" % RO][:], ["OUTT"], ["TB%d" % RO], scale=0.5)
    dma("s", 4, T.yt[:], T.OUTT[:], ["OUTT"], ["yt"])
    for i in range(16):
        MM(T.bk0[:, 0:C], T.mI[:], T.U[:, i:W:16], i == 0, i == 15, "bk0", ["mI", "U"])
    V("cp", T.OUTC[:], ["OUTC"], ["bk0"], T.bk0[:, 0:C])
    dma("y", 5, T.yc[:], T.OUTC[:], ["OUTC"], ["yc"])
    need("y", "dma4", 16)
    need("y", "dma5", 16)
    g.wait_ge(T.sem["snd"], sum(len(topo.engines(core, T.cores[(rank + (1 if t < RO - 1 else 1 - RO)) % N])) for t in range(RO)))
